import numpy as np
import ml_dtypes


def mxq(x, axis, fmt="e4m3"):
    dtype, down = {"e4m3": (ml_dtypes.float8_e4m3fn, 7), "e5m2": (ml_dtypes.float8_e5m2, 14)}[fmt]
    v = np.moveaxis(np.asarray(x, np.float32).astype(ml_dtypes.bfloat16).astype(np.float64), axis, -1)
    blocks = v.reshape(v.shape[:-1] + (-1, 32))
    amax = np.abs(blocks).max(-1, keepdims=True)
    byte = np.maximum(np.where(amax > 0, np.frexp(amax)[1] - 1 + 127, 0) - down, 1)
    scale = np.exp2(byte - 127.0)
    codes = (blocks / scale).astype(np.float32).astype(dtype).astype(np.float64)
    return np.moveaxis((codes * scale).reshape(v.shape), -1, axis)


WIDE = False


def mx_kscale(k):
    if not WIDE:
        return np.ones(k)
    levels = np.array([10, -10, 5, -5, 0])
    if k % 512:
        return np.exp2(np.random.permutation(np.resize(levels, k // 32))).repeat(32)
    a = np.empty((k // 512, 16))
    for p in range(k // 512):
        a[p, :8] = np.random.permutation(np.resize(levels, 8))
        for g in range(8):
            far = levels[np.abs(levels - a[p, g]) >= 10]
            a[p, g + 8] = far[np.random.randint(len(far))]
    return np.exp2(a.ravel()).repeat(32)


BF16 = ml_dtypes.bfloat16


def bf(x):
    return np.asarray(x, np.float32).astype(BF16)


def f64(x):
    return np.asarray(x).astype(np.float64)


E2M1 = np.array([0.0, 0.5, 1.0, 1.5, 2.0, 3.0, 4.0, 6.0, -0.0, -0.5, -1.0, -1.5, -2.0, -3.0, -4.0, -6.0])


def pack_weight(w, fmt):
    k, n = w.shape
    w = f64(bf(w)).reshape(k // 32, 32, n)
    amax = np.abs(w).max(1)
    if fmt == "e4m3":
        byte = np.frexp(amax)[1] - 1 + 127 - 7
    else:
        mant, ex = np.frexp(amax / 6.0)
        byte = np.where(mant > 0.5, ex, ex - 1) + 127
    byte = np.clip(np.where(amax > 0, byte, 1), 1, 254)
    scaled = (w * np.exp2(127.0 - byte)[:, None, :]).reshape(k, n).astype(np.float32)
    by_word = np.ascontiguousarray(scaled.reshape(k // 512, 128, 4, n).transpose(0, 1, 3, 2))
    if fmt == "e4m3":
        words = by_word.astype(ml_dtypes.float8_e4m3fn).view(np.uint8)
    else:
        c = by_word.astype(ml_dtypes.float4_e2m1fn).view(np.uint8) & 0xF
        words = c[..., 0::2] | (c[..., 1::2] << 4)
    return np.ascontiguousarray(words), np.ascontiguousarray(byte.astype(np.uint8).reshape(k // 512, 16, n))


def unpack_weight(words, scales, fmt):
    g, p, n, _ = words.shape
    if fmt == "e4m3":
        vals = np.ascontiguousarray(words).view(ml_dtypes.float8_e4m3fn).astype(np.float64)
    else:
        nib = np.empty((g, p, n, 4), np.uint8)
        nib[..., 0::2] = words & 0xF
        nib[..., 1::2] = words >> 4
        vals = E2M1[nib]
    vals = vals * np.repeat(np.exp2(scales.astype(np.float64) - 127.0), 8, axis=1)[..., None]
    return vals.transpose(0, 1, 3, 2).reshape(g * 512, n)
def pack4(w):
    words, scales = pack_weight(w, "e2m1")
    return words.reshape(words.shape[0], 128, -1), scales


def unpack4(words, scales):
    return unpack_weight(words.reshape(words.shape[0], 128, -1, 2), scales, "e2m1")


T, D, E = 1536, 1024, 1024


def draw0():
    s, u = mx_kscale(D), mx_kscale(D)
    t = mx_kscale(T)
    words, scales = pack4(0.8 * np.random.standard_normal((D, E)) / np.sqrt(D) / s[:, None])
    query_a = np.random.standard_normal((T, D)) * s
    query_b = np.random.standard_normal((T, D)) * u
    keys_b = 0.8 * np.random.standard_normal((D, E)) / np.sqrt(D) / u[:, None]
    signed = np.random.standard_normal(T) / T ** 0.25
    positive = np.exp(0.3 * np.random.standard_normal(T)) / T ** 0.25
    return {"query_a": bf(query_a),
            "query_b": bf(query_b),
            "keys_a_words": words,
            "keys_a_scales": scales,
            "keys_b": bf(keys_b),
            "coef": bf(np.stack([signed * t, positive / t]))}


def core(query_a, query_b, keys_a_words, keys_a_scales, keys_b, coef):
    keys_a = unpack4(keys_a_words, keys_a_scales)
    score_a = mxq(f64(query_a), 1, "e4m3") @ keys_a
    score_b = mxq(f64(query_b), 1, "e4m3") @ mxq(f64(keys_b), 0, "e4m3")
    p = np.exp(np.stack([score_a, score_b])) * f64(coef)[:, :, None]
    credit = mxq(p[0], 0, "e4m3").T @ mxq(p[1], 0, "e4m3")
    return credit


def e4m3fn_bytes(y):
    return np.clip(np.asarray(y, np.float64), -448.0, 448.0).astype(np.float32).astype(ml_dtypes.float8_e4m3fn).view(np.uint8)


def e4m3fn_values(b):
    return np.asarray(b, np.uint8).view(ml_dtypes.float8_e4m3fn).astype(np.float64)


def setup_inputs():
    d = draw0()
    x0 = np.asarray(d['query_b']).astype(np.float64)
    s = (np.max(np.abs(x0), axis=(0,), keepdims=True) / 448.0).astype(np.float32)
    out = {}
    for k, v in d.items():
        if k == 'query_b':
            out['query_b_bytes'] = e4m3fn_bytes(x0 / s.astype(np.float64))
            out['query_b_scale'] = s
        else:
            out[k] = v
    return out


def reference(query_a, query_b_bytes, query_b_scale, keys_a_words, keys_a_scales, keys_b, coef):
    return core(query_a, e4m3fn_values(query_b_bytes) * query_b_scale.astype(np.float64), keys_a_words, keys_a_scales, keys_b, coef)

@@ -1,0 +1,320 @@
+from contextlib import ExitStack
+
+import concourse.mybir as mybir
+from concourse.masks import make_identity
+
+T, D, E = 1536, 1024, 1024
+P = 128
+GROUPS = 3
+BLOCKS = [[(0, 512), (512, 512)], [(0, 512), (512, 256), (768, 256)]]
+FLOPS = 3 * 2 * T * D * E
+
+F32 = mybir.dt.float32
+BF16 = mybir.dt.bfloat16
+U32 = mybir.dt.uint32
+I32 = mybir.dt.int32
+U8 = mybir.dt.uint8
+FP8 = mybir.dt.float8_e4m3fn
+E4M3X4 = mybir.dt.float8_e4m3fn_x4
+E2M1X4 = mybir.dt.float4_e2m1fn_x4
+ACT = mybir.ActivationFunctionType
+ALU = mybir.AluOpType
+
+
+ORDER = """
+i00v j00 p00 i10s t000s t001s t100s p01 p02 t101s t002s p03 t003s q100 p10 q000 t102s j10 t103s p11
+t010v i01s t110s p12 s0000 s1000 q001 t111s t011s s0001 q101 p13 s1001 t012s q110 t112s t013s s0002
+q010 s0003 p20 t113s p21 q011 q111 t020s t021s s0010 s1002 t022s w000 s1003 s1010 p22 s0011 w100 p23
+t023s t120s t121v j01 x000 i11s s0012 x100 t122s t123v s1011 s1012 q020 s1013 q120 q021 s0013 s1020
+s0020 s1021 s0021 q121 s0022 s1022 j11 s0023 s0100 s0101 s0102 w001 s0103 s1023 w101 x001 s0110 w002
+x101 s1100 s0111 w102 s0112 x002 s1101 s0113 x102 s0120 s1102 w010 s1103 s1110 s0121 s1111 c00s
+s0122 w011 c10s w110 s0123 s1112 x010 s1113 s1120 w012 s1121 s1122 s1123 c20s w111 s1200 x011 s1201
+c30s x012 s1202 s1203 s1210 s1211 w112 s1212 x110 s1213 w120 s1220 s1221 s1222 w121 s1223 c40s c50s
+x111 x112 c60v w122 c70s c01v c11v x120 c21s c31s x121 c41v x122 c51s c61s c71s c02v c12v c22s c32v
+c42s c52v c62v c72s
+"""
+
+
+def tile_product_key_credit_s11_kernel(
+    tc, query_a, query_b_bytes, query_b_scale, keys_a_words, keys_a_scales, keys_b, coef, out
+):
+    nc = tc.nc
+    with ExitStack() as ctx:
+        keep = ctx.enter_context(tc.tile_pool(name="keep", bufs=1))
+        work = ctx.enter_context(tc.tile_pool(name="work", bufs=2))
+        psum = ctx.enter_context(tc.psum_pool(name="psum", bufs=1))
+
+        ident = keep.tile([P, P], F32, name="ident")
+        srows = keep.tile([P, P], F32, name="srows")
+        scol = keep.tile([P, 8], F32, name="scol")
+        sbc = keep.tile([P, D], F32, name="sbc", align_bytes=64)
+        coef_raw = keep.tile([P, 6, 4], BF16, name="coef_raw")
+        coef_f = keep.tile([P, 24], F32, name="coef_f")
+        gt = keep.tile([P, 12], F32, name="gt")
+        lt = keep.tile([P, 12], F32, name="lt")
+        lnb = keep.tile([P, 12], F32, name="lnb")
+        mag = keep.tile([P, 12], F32, name="mag")
+        ca = keep.tile([P, 12], F32, name="ca")
+        kaw = keep.tile([P, 2, 2048], U8, name="kaw", align_bytes=64)
+        kas = keep.tile([P, 2, 1024], U8, name="kas", align_bytes=64)
+        kbc = keep.tile([P, 2, 1024], U32, name="kbc", align_bytes=64)
+        kbs = keep.tile([P, 2, 1024], U8, name="kbs", align_bytes=64)
+        pac = keep.tile([P, GROUPS, E], U32, name="pac", align_bytes=64)
+        pas = keep.tile([P, GROUPS, E], U8, name="pas", align_bytes=64)
+        pbc = keep.tile([P, GROUPS, E], U32, name="pbc", align_bytes=64)
+        pbs = keep.tile([P, GROUPS, E], U8, name="pbs", align_bytes=64)
+        qac = [keep.tile([P, 4, 2, P], U32, name="qac%d" % g, align_bytes=64) for g in range(GROUPS)]
+        qas = [keep.tile([P, 4, 2, P], U8, name="qas%d" % g, align_bytes=64) for g in range(GROUPS)]
+        qbc = [keep.tile([P, 4, 2, P], U32, name="qbc%d" % g, align_bytes=64) for g in range(GROUPS)]
+        qbs = [keep.tile([P, 4, 2, P], U8, name="qbs%d" % g, align_bytes=64) for g in range(GROUPS)]
+        qbb = [keep.tile([P, 4, D], U8, name="qbb%d" % g, align_bytes=64) for g in range(GROUPS)]
+        kbr = {
+            (g, h): keep.tile([P, 4, 512], BF16, name="kbr%d%d" % (g, h), align_bytes=64)
+            for h in range(2)
+            for g in range(2)
+        }
+
+        make_identity(nc, ident[:])
+        nc.vector.memset(srows[:], 0.0)
+        nc.vector.memset(kas[:].rearrange("p g n -> p (g n)").bitcast(I32), 0)
+        nc.scalar.dma_start(out=coef_raw[:], in_=coef.rearrange("s (g p t) -> p (s g) t", p=P, t=4))
+        nc.sync.dma_start(out=srows[0:8, :], in_=query_b_scale.rearrange("o (m n) -> (o m) n", n=P))
+
+        qa_view = query_a.rearrange("(g p t) d -> g p t d", p=P, t=4)
+        qb_view = query_b_bytes.rearrange("(g p t) d -> g p t d", p=P, t=4)
+        qar = {}
+
+        def load_qa(g, t):
+            qar[g, t] = work.tile([P, D], BF16, name="qar", tag="qar", bufs=12, align_bytes=64)
+            nc.sync.dma_start(out=qar[g, t][:], in_=qa_view[g][:, t, :])
+
+        def load_qb(g):
+            nc.sync.dma_start(out=qbb[g][:], in_=qb_view[g])
+
+        kb_view = keys_b.rearrange("(g p t) n -> g p t n", p=P, t=4)
+
+        def load_ka():
+            nc.sync.dma_start(out=kaw[:], in_=keys_a_words.rearrange("g p x -> p g x"))
+
+        def load_kas():
+            for q in range(4):
+                nc.sync.dma_start(
+                    out=kas[32 * q : 32 * q + 4, :, :].bitcast(I32),
+                    in_=keys_a_scales[:, 4 * q : 4 * q + 4, :].rearrange("g r n -> r g n").bitcast(I32),
+                )
+
+        def load_kb(g, h):
+            nc.sync.dma_start(out=kbr[g, h][:], in_=kb_view[g][:, :, 512 * h : 512 * h + 512])
+
+        load_kb(0, 0)
+        load_kb(1, 0)
+        load_kas()
+        load_qb(0)
+        load_qa(0, 0)
+        load_qa(0, 1)
+        load_qa(0, 2)
+        load_qa(0, 3)
+        load_qb(1)
+        load_ka()
+        load_kb(0, 1)
+        load_qa(1, 0)
+        load_qa(1, 1)
+        load_kb(1, 1)
+        load_qa(1, 2)
+        load_qa(1, 3)
+        load_qa(2, 0)
+        load_qa(2, 1)
+        load_qa(2, 2)
+        load_qb(2)
+        load_qa(2, 3)
+
+        nc.vector.tensor_copy(out=coef_f[:], in_=coef_raw[:].rearrange("p x t -> p (x t)"))
+        cb = coef_f[:, 12:24]
+        nc.vector.tensor_scalar(out=gt[:], in0=cb, scalar1=0.0, scalar2=None, op0=ALU.is_gt)
+        nc.vector.tensor_scalar(out=lt[:], in0=cb, scalar1=0.0, scalar2=None, op0=ALU.is_lt)
+        nc.vector.tensor_tensor(out=gt[:], in0=gt[:], in1=lt[:], op=ALU.subtract)
+        nc.vector.tensor_tensor(out=mag[:], in0=cb, in1=gt[:], op=ALU.mult)
+        nc.vector.tensor_scalar(out=mag[:], in0=mag[:], scalar1=1e-19, scalar2=None, op0=ALU.max)
+        nc.vector.tensor_tensor(out=ca[:], in0=coef_f[:, 0:12], in1=gt[:], op=ALU.mult)
+        nc.scalar.activation(out=lnb[:], in_=mag[:], func=ACT.Ln)
+
+        def bank(tag, bufs, name):
+            return psum.tile([P, 512], F32, name=name, tag=tag, bufs=bufs)
+
+        TP, MM = 3, 5
+        b0 = bank("tp", TP, "b0")
+        nc.tensor.transpose(b0[:, 0:P], srows[:], ident[:])
+        nc.vector.tensor_copy(out=scol[:], in_=b0[:, 0:8])
+        for half in range(2):
+            bb = bank("tp", TP, "bb")
+            for j in range(4):
+                m = 4 * half + j
+                nc.tensor.transpose(
+                    bb[:, P * j : P * j + P], scol[:, m : m + 1].to_broadcast([P, P]), ident[:]
+                )
+            nc.vector.tensor_copy(out=sbc[:, 512 * half : 512 * half + 512], in_=bb[:])
+
+        prod = {}
+
+        def product(g, t):
+            w = work.tile([P, D], BF16, name="prod", tag="prod", bufs=6, align_bytes=64)
+            nc.vector.tensor_tensor(out=w[:], in0=qbb[g][:, t, :].bitcast(FP8), in1=sbc[:], op=ALU.mult)
+            prod[g, t] = w
+
+        grp = {}
+
+        def turn(side, g, t, engine):
+            src = qar[g, t][:] if side == 0 else prod[g, t][:]
+            words = src.bitcast(F32)
+            b = bank("tp", TP, "tb")
+            for c in range(2):
+                for u in range(2):
+                    j = 2 * c + u
+                    nc.tensor.transpose(
+                        b[:, P * j : P * j + P], words[:, 256 * c + u : 256 * c + 256 : 2], ident[:]
+                    )
+            if (side, g, t // 2) not in grp:
+                grp[side, g, t // 2] = work.tile(
+                    [P, 2, 2, P, 2], F32, name="grp", tag="grp", bufs=4, align_bytes=64
+                )
+            dst = grp[side, g, t // 2][:, t % 2, :, :, :]
+            srcb = b[:].rearrange("p (c u r) -> p c r u", c=2, u=2)
+            if engine == "s":
+                nc.scalar.copy(out=dst, in_=srcb)
+            else:
+                nc.vector.tensor_copy(out=dst, in_=srcb)
+
+        def quant_q(side, g, pair):
+            codes, scales = (qac[g], qas[g]) if side == 0 else (qbc[g], qbs[g])
+            nc.vector.quantize_mx(
+                out=codes[:, 2 * pair : 2 * pair + 2, :, :].rearrange("p a c r -> p (a c r)").bitcast(E4M3X4),
+                scales=scales[:, 2 * pair : 2 * pair + 2, :, :].rearrange("p a c r -> p (a c r)"),
+                in_=grp[side, g, pair][:].rearrange("p a c r u -> p (a c r u)").bitcast(BF16),
+            )
+
+        kbg = {}
+
+        def kb_inter(c, h, engine):
+            w = work.tile([P, 512, 4], BF16, name="kbg", tag="kbg", bufs=2, align_bytes=64)
+            src = kbr[c, h][:].rearrange("p t n -> p n t")
+            if engine == "s":
+                nc.scalar.copy(out=w[:], in_=src)
+            else:
+                nc.vector.tensor_copy(out=w[:], in_=src)
+            kbg[c, h] = w
+
+        def kb_quant(c, h):
+            nc.vector.quantize_mx(
+                out=kbc[:, c, 512 * h : 512 * h + 512].bitcast(E4M3X4),
+                scales=kbs[:, c, 512 * h : 512 * h + 512],
+                in_=kbg[c, h][:].rearrange("p n t -> p (n t)"),
+            )
+
+        ea, eb = {}, {}
+
+        def score(side, bi, g, t):
+            s0, w = BLOCKS[side][bi]
+            b = bank("mm", MM, "sc")
+            codes, scales = (qac, qas) if side == 0 else (qbc, qbs)
+            for c in range(2):
+                if side == 0:
+                    rhs = kaw[:, c, 2 * s0 : 2 * s0 + 2 * w].bitcast(E2M1X4)
+                    rsc = kas[:, c, s0 : s0 + w]
+                else:
+                    rhs = kbc[:, c, s0 : s0 + w].bitcast(E4M3X4)
+                    rsc = kbs[:, c, s0 : s0 + w]
+                nc.tensor.matmul_mx(
+                    out=b[:, 0:w],
+                    lhsT=codes[g][:, t, c, :].bitcast(E4M3X4),
+                    lhsT_scale=scales[g][:, t, c, :],
+                    rhs=rhs,
+                    rhs_scale=rsc,
+                    start=(c == 0),
+                    stop=(c == 1),
+                )
+            store = ea if side == 0 else eb
+            if (bi, g) not in store:
+                if side == 0:
+                    store[bi, g] = work.tile([P, 4, w], F32, name="ea", tag="ea", bufs=3)
+                else:
+                    store[bi, g] = work.tile([P, 4, w], BF16, name="eb", tag="eb", bufs=3)
+            k = 4 * g + t
+            if side == 0:
+                nc.scalar.activation(out=store[bi, g][:, t, :], in_=b[:, 0:w], func=ACT.Exp)
+            else:
+                nc.scalar.activation(
+                    out=store[bi, g][:, t, :], in_=b[:, 0:w], func=ACT.Exp, bias=lnb[:, k : k + 1]
+                )
+
+        pg = {}
+
+        def weigh(side, bi, g):
+            w = BLOCKS[side][bi][1]
+            o = work.tile([P, w, 4], BF16, name="pg", tag="pg", bufs=4, align_bytes=64)
+            e = (ea if side == 0 else eb)[bi, g][:].rearrange("p t n -> p n t")
+            if side == 0:
+                nc.vector.tensor_tensor(
+                    out=o[:],
+                    in0=e,
+                    in1=ca[:, 4 * g : 4 * g + 4].unsqueeze(1).to_broadcast([P, w, 4]),
+                    op=ALU.mult,
+                )
+            else:
+                nc.vector.tensor_copy(out=o[:], in_=e)
+            pg[side, bi, g] = o
+
+        def quant_p(side, bi, g):
+            s0, w = BLOCKS[side][bi]
+            codes, scales = (pac, pas) if side == 0 else (pbc, pbs)
+            nc.vector.quantize_mx(
+                out=codes[:, g, s0 : s0 + w].bitcast(E4M3X4),
+                scales=scales[:, g, s0 : s0 + w],
+                in_=pg[side, bi, g][:].rearrange("p n t -> p (n t)"),
+            )
+
+        def credit(i, bi, engine):
+            s0, w = BLOCKS[1][bi]
+            b = bank("mm", MM, "cr")
+            for g in range(GROUPS):
+                nc.tensor.matmul_mx(
+                    out=b[:, 0:w],
+                    lhsT=pac[:, g, P * i : P * i + P].bitcast(E4M3X4),
+                    lhsT_scale=pas[:, g, P * i : P * i + P],
+                    rhs=pbc[:, g, s0 : s0 + w].bitcast(E4M3X4),
+                    rhs_scale=pbs[:, g, s0 : s0 + w],
+                    start=(g == 0),
+                    stop=(g == GROUPS - 1),
+                )
+            o = work.tile([P, w], F32, name="o", tag="o", bufs=4)
+            if engine == "s":
+                nc.scalar.copy(out=o[:], in_=b[:, 0:w])
+            else:
+                nc.vector.tensor_copy(out=o[:], in_=b[:, 0:w])
+            nc.sync.dma_start(out=out[P * i : P * i + P, s0 : s0 + w], in_=o[:])
+
+        def emit(u):
+            k = u[0]
+            a = [int(x) for x in u[1:] if x in "0123456789"]
+            e = u[-1]
+            if k == "p":
+                product(*a)
+            elif k == "t":
+                turn(a[0], a[1], a[2], e)
+            elif k == "q":
+                quant_q(*a)
+            elif k == "i":
+                kb_inter(a[0], a[1], e)
+            elif k == "j":
+                kb_quant(*a)
+            elif k == "s":
+                score(*a)
+            elif k == "w":
+                weigh(*a)
+            elif k == "x":
+                quant_p(*a)
+            elif k == "c":
+                credit(a[0], a[1], e)
+
+        with tc.manual_schedule():
+            for u in ORDER.split():
+                emit(u)

@@ -22,16 +22,16 @@ ALU = mybir.AluOpType
 
 
 ORDER = """
-i00v j00 p00 i10s t000s t001s t100s p01 p02 t101s t002s p03 t003s q100 p10 q000 t102s j10 t103s p11
-t010v i01s t110s p12 s0000 s1000 q001 t111s t011s s0001 q101 p13 s1001 t012s q110 t112s t013s s0002
-q010 s0003 p20 t113s p21 q011 q111 t020s t021s s0010 s1002 t022s w000 s1003 s1010 p22 s0011 w100 p23
-t023s t120s t121v j01 x000 i11s s0012 x100 t122s t123v s1011 s1012 q020 s1013 q120 q021 s0013 s1020
-s0020 s1021 s0021 q121 s0022 s1022 j11 s0023 s0100 s0101 s0102 w001 s0103 s1023 w101 x001 s0110 w002
-x101 s1100 s0111 w102 s0112 x002 s1101 s0113 x102 s0120 s1102 w010 s1103 s1110 s0121 s1111 c00s
-s0122 w011 c10s w110 s0123 s1112 x010 s1113 s1120 w012 s1121 s1122 s1123 c20s w111 s1200 x011 s1201
-c30s x012 s1202 s1203 s1210 s1211 w112 s1212 x110 s1213 w120 s1220 s1221 s1222 w121 s1223 c40s c50s
-x111 x112 c60v w122 c70s c01v c11v x120 c21s c31s x121 c41v x122 c51s c61s c71s c02v c12v c22s c32v
-c42s c52v c62v c72s
+i00v t000s t001s t002s j00 t003s t010s p00 p01 t100s q000 t101s t011s p02 s0000 s0001 q001 s0002 p03
+q100 t012s p10 t013s p11 t102s i10v s0003 q010 p12 i01s j10 p13 t103s t020s t110s q011 p20 q101
+t111s t112s t021s w000 j01 s0010 q110 t113s i11s s0011 q111 q020 s1000 t022s t023v s1001 p21 x000
+s0012 s0013 q021 t120s s0020 s1002 s0021 t121s s0022 p22 s0023 p23 w001 q120 t122s s0100 s1003 w002
+s1010 s0101 s1011 j11 s1012 s0102 t123v x001 s1013 s0103 s1020 q121 s0110 s1021 w100 s0111 s0112
+w010 s1022 x100 x002 s1023 s0113 s0120 s1100 w101 s1101 s0121 w102 x101 s1102 s1103 s0122 x010 s1110
+s1111 s0123 s1112 w110 s1113 s1120 x102 s1121 w011 s1122 s1123 w111 w012 s1200 c00s s1201 s1202
+s1203 x011 x012 c10s s1210 c20s s1211 x110 w112 s1212 s1213 c30s s1220 s1221 w120 s1222 c40s c50s
+x111 x112 w121 c60v c70s x120 x121 c01s s1223 c11v c21s c31s c41s w122 x122 c51s c61v c71s c02v c12v
+c22s c32v c42s c52v c62s c72v
 """
 
 
@@ -48,7 +48,9 @@ def tile_product_key_credit_s11_kernel(
         srows = keep.tile([P, P], F32, name="srows")
         scol = keep.tile([P, 8], F32, name="scol")
         sbc = keep.tile([P, D], F32, name="sbc", align_bytes=64)
-        coef_raw = keep.tile([P, 6, 4], BF16, name="coef_raw")
+        crows = keep.tile([P, 2 * P], F32, name="crows")
+        warm = keep.tile([P, 512], BF16, name="warm")
+        junk = keep.tile([P, 1], F32, name="junk")
         coef_f = keep.tile([P, 24], F32, name="coef_f")
         gt = keep.tile([P, 12], F32, name="gt")
         lt = keep.tile([P, 12], F32, name="lt")
@@ -74,10 +76,14 @@ def tile_product_key_credit_s11_kernel(
             for g in range(2)
         }
 
-        make_identity(nc, ident[:])
+        nc.vector.memset(warm[:], 0.0)
+        nc.vector.memset(crows[:], 0.0)
         nc.vector.memset(srows[:], 0.0)
         nc.vector.memset(kas[:].rearrange("p g n -> p (g n)").bitcast(I32), 0)
-        nc.scalar.dma_start(out=coef_raw[:], in_=coef.rearrange("s (g p t) -> p (s g) t", p=P, t=4))
+        make_identity(nc, ident[:])
+        nc.scalar.dma_start(
+            out=crows[0:6, :].bitcast(BF16), in_=coef.rearrange("s (g m) -> (s g) m", m=512)
+        )
         nc.sync.dma_start(out=srows[0:8, :], in_=query_b_scale.rearrange("o (m n) -> (o m) n", n=P))
 
         qa_view = query_a.rearrange("(g p t) d -> g p t d", p=P, t=4)
@@ -107,52 +113,70 @@ def tile_product_key_credit_s11_kernel(
             nc.sync.dma_start(out=kbr[g, h][:], in_=kb_view[g][:, :, 512 * h : 512 * h + 512])
 
         load_kb(0, 0)
-        load_kb(1, 0)
-        load_kas()
-        load_qb(0)
         load_qa(0, 0)
+        load_kas()
         load_qa(0, 1)
+        load_qb(0)
         load_qa(0, 2)
         load_qa(0, 3)
-        load_qb(1)
-        load_ka()
-        load_kb(0, 1)
         load_qa(1, 0)
         load_qa(1, 1)
-        load_kb(1, 1)
         load_qa(1, 2)
+        load_ka()
+        load_qb(1)
         load_qa(1, 3)
+        load_kb(1, 0)
         load_qa(2, 0)
         load_qa(2, 1)
+        load_kb(0, 1)
         load_qa(2, 2)
+        load_kb(1, 1)
         load_qb(2)
         load_qa(2, 3)
-
-        nc.vector.tensor_copy(out=coef_f[:], in_=coef_raw[:].rearrange("p x t -> p (x t)"))
-        cb = coef_f[:, 12:24]
-        nc.vector.tensor_scalar(out=gt[:], in0=cb, scalar1=0.0, scalar2=None, op0=ALU.is_gt)
-        nc.vector.tensor_scalar(out=lt[:], in0=cb, scalar1=0.0, scalar2=None, op0=ALU.is_lt)
-        nc.vector.tensor_tensor(out=gt[:], in0=gt[:], in1=lt[:], op=ALU.subtract)
-        nc.vector.tensor_tensor(out=mag[:], in0=cb, in1=gt[:], op=ALU.mult)
-        nc.vector.tensor_scalar(out=mag[:], in0=mag[:], scalar1=1e-19, scalar2=None, op0=ALU.max)
-        nc.vector.tensor_tensor(out=ca[:], in0=coef_f[:, 0:12], in1=gt[:], op=ALU.mult)
-        nc.scalar.activation(out=lnb[:], in_=mag[:], func=ACT.Ln)
 
         def bank(tag, bufs, name):
             return psum.tile([P, 512], F32, name=name, tag=tag, bufs=bufs)
 
         TP, MM = 3, 5
-        b0 = bank("tp", TP, "b0")
-        nc.tensor.transpose(b0[:, 0:P], srows[:], ident[:])
-        nc.vector.tensor_copy(out=scol[:], in_=b0[:, 0:8])
-        for half in range(2):
-            bb = bank("tp", TP, "bb")
-            for j in range(4):
-                m = 4 * half + j
-                nc.tensor.transpose(
-                    bb[:, P * j : P * j + P], scol[:, m : m + 1].to_broadcast([P, P]), ident[:]
-                )
-            nc.vector.tensor_copy(out=sbc[:, 512 * half : 512 * half + 512], in_=bb[:])
+        wbank = bank("mm", MM, "wbank")
+
+        def warm_up():
+            nc.tensor.matmul(wbank[:], lhsT=warm[:, 0:P], rhs=warm[:], start=True, stop=True)
+
+        def head():
+            for i in range(4):
+                warm_up()
+            b0 = bank("tp", TP, "b0")
+            for u in range(2):
+                nc.tensor.transpose(b0[:, P * u : P * u + P], crows[:, u::2], ident[:])
+            nc.tensor.transpose(b0[:, 2 * P : 3 * P], srows[:], ident[:])
+            nc.vector.tensor_copy(out=scol[:], in_=b0[:, 2 * P : 2 * P + 8])
+            nc.vector.tensor_copy(
+                out=coef_f[:].rearrange("p (x u e) -> p u x e", x=6, u=2),
+                in_=b0[:, 0 : 2 * P].bitcast(BF16).rearrange("p (u r e) -> p u r e", u=2, e=2)[:, :, 0:6, :],
+            )
+            banks = []
+            for half in range(2):
+                bb = bank("tp", TP, "bb")
+                for j in range(4):
+                    m = 4 * half + j
+                    nc.tensor.transpose(
+                        bb[:, P * j : P * j + P], scol[:, m : m + 1].to_broadcast([P, P]), ident[:]
+                    )
+                banks.append(bb)
+            cb = coef_f[:, 12:24]
+            nc.vector.scalar_tensor_tensor(
+                out=mag[:], in0=cb, scalar=-1.0, in1=cb, op0=ALU.mult, op1=ALU.max
+            )
+            nc.vector.tensor_copy(out=sbc[:, 0:512], in_=banks[0][:])
+            nc.vector.tensor_scalar(out=mag[:], in0=mag[:], scalar1=1e-19, scalar2=None, op0=ALU.max)
+            nc.scalar.activation(out=lnb[:], in_=mag[:], func=ACT.Ln)
+            nc.scalar.activation(out=junk[:], in_=lnb[:, 0:1], func=ACT.Exp)
+            nc.vector.tensor_copy(out=sbc[:, 512:1024], in_=banks[1][:])
+            nc.gpsimd.tensor_scalar(out=gt[:], in0=cb, scalar1=0.0, scalar2=None, op0=ALU.is_gt)
+            nc.gpsimd.tensor_scalar(out=lt[:], in0=cb, scalar1=0.0, scalar2=None, op0=ALU.is_lt)
+            nc.gpsimd.tensor_tensor(out=gt[:], in0=gt[:], in1=lt[:], op=ALU.subtract)
+            nc.gpsimd.tensor_tensor(out=ca[:], in0=coef_f[:, 0:12], in1=gt[:], op=ALU.mult)
 
         prod = {}
 
@@ -196,11 +220,12 @@ def tile_product_key_credit_s11_kernel(
 
         def kb_inter(c, h, engine):
             w = work.tile([P, 512, 4], BF16, name="kbg", tag="kbg", bufs=2, align_bytes=64)
-            src = kbr[c, h][:].rearrange("p t n -> p n t")
+            dst = w[:].rearrange("p (c i) t -> p c t i", i=4)
+            src = kbr[c, h][:].rearrange("p t (c i) -> p c t i", i=4)
             if engine == "s":
-                nc.scalar.copy(out=w[:], in_=src)
+                nc.scalar.copy(out=dst, in_=src)
             else:
-                nc.vector.tensor_copy(out=w[:], in_=src)
+                nc.vector.tensor_copy(out=dst, in_=src)
             kbg[c, h] = w
 
         def kb_quant(c, h):
@@ -251,16 +276,17 @@ def tile_product_key_credit_s11_kernel(
         def weigh(side, bi, g):
             w = BLOCKS[side][bi][1]
             o = work.tile([P, w, 4], BF16, name="pg", tag="pg", bufs=4, align_bytes=64)
-            e = (ea if side == 0 else eb)[bi, g][:].rearrange("p t n -> p n t")
+            e = (ea if side == 0 else eb)[bi, g][:].rearrange("p t (c i) -> p c t i", i=4)
+            dst = o[:].rearrange("p (c i) t -> p c t i", i=4)
             if side == 0:
                 nc.vector.tensor_tensor(
-                    out=o[:],
+                    out=dst,
                     in0=e,
-                    in1=ca[:, 4 * g : 4 * g + 4].unsqueeze(1).to_broadcast([P, w, 4]),
+                    in1=ca[:, 4 * g : 4 * g + 4].unsqueeze(1).unsqueeze(3).to_broadcast([P, w // 4, 4, 4]),
                     op=ALU.mult,
                 )
             else:
-                nc.vector.tensor_copy(out=o[:], in_=e)
+                nc.vector.tensor_copy(out=dst, in_=e)
             pg[side, bi, g] = o
 
         def quant_p(side, bi, g):
@@ -316,5 +342,12 @@ def tile_product_key_credit_s11_kernel(
                 credit(a[0], a[1], e)
 
         with tc.manual_schedule():
+            head()
+            turns, scored = 0, False
             for u in ORDER.split():
                 emit(u)
+                scored = scored or u[0] == "s"
+                if u[0] == "t" and not scored:
+                    turns += 1
+                    if turns % 2 == 0:
+                        warm_up()

@@ -6,7 +6,6 @@ from concourse.masks import make_identity
 T, D, E = 1536, 1024, 1024
 P = 128
 GROUPS = 3
-BLOCKS = [[(0, 512), (512, 512)], [(0, 512), (512, 256), (768, 256)]]
 FLOPS = 3 * 2 * T * D * E
 
 F32 = mybir.dt.float32
@@ -20,18 +19,16 @@ E2M1X4 = mybir.dt.float4_e2m1fn_x4
 ACT = mybir.ActivationFunctionType
 ALU = mybir.AluOpType
 
-
+LOADS = "a00A k00 b0 k10 a01 b1 a10 a11 a20 k01 x b2 w a21 k11A"
 ORDER = """
-i00v t000s t001s t002s j00 t003s t010s p00 p01 t100s q000 t101s t011s p02 s0000 s0001 q001 s0002 p03
-q100 t012s p10 t013s p11 t102s i10v s0003 q010 p12 i01s j10 p13 t103s t020s t110s q011 p20 q101
-t111s t112s t021s w000 j01 s0010 q110 t113s i11s s0011 q111 q020 s1000 t022s t023v s1001 p21 x000
-s0012 s0013 q021 t120s s0020 s1002 s0021 t121s s0022 p22 s0023 p23 w001 q120 t122s s0100 s1003 w002
-s1010 s0101 s1011 j11 s1012 s0102 t123v x001 s1013 s0103 s1020 q121 s0110 s1021 w100 s0111 s0112
-w010 s1022 x100 x002 s1023 s0113 s0120 s1100 w101 s1101 s0121 w102 x101 s1102 s1103 s0122 x010 s1110
-s1111 s0123 s1112 w110 s1113 s1120 x102 s1121 w011 s1122 s1123 w111 w012 s1200 c00s s1201 s1202
-s1203 x011 x012 c10s s1210 c20s s1211 x110 w112 s1212 s1213 c30s s1220 s1221 w120 s1222 c40s c50s
-x111 x112 w121 c60v c70s x120 x121 c01s s1223 c11v c21s c31s c41s w122 x122 c51s c61v c71s c02v c12v
-c22s c32v c42s c52v c62s c72v
+t000v t001v i00s p00 i10s t100s t002s p01 p02 t101s t003s t010s t102s p03 t011s p10 t103s p11 t012s
+p12 q000 t110s p13 t013s q100 t111s j0 p20 q010 t112s t020s p21 t021s t113s s0000 s1000 p22 p23
+s1001 s0001 s0002 i01v s1002 s0003 s1003 s0010 t120s t022s t023s q110 i11v w100 t121s q020 t122s
+t123s s0011 q120 s1010 s1011 s0012 s0013 s1012 s0020 s1013 w000 s1020 s1021 s1022 s0021 s0022 j1
+s1023 x100 s0023 s0100 w101 s1100 s0110 s1101 x000 w001 s1102 w102 w002 s1103 s0120 x101 s0200 s1110
+x001 s1111 s0210 s1112 s1113 s1120 w110 s1121 s0220 s1122 x002 x102 w111 s1123 s0300 w010 s0310 x110
+c00s c10s s0320 s0400 w112 c20s x111 c30s s0410 x112 s0420 x010 c01s w020 x011 w030 x020 x021 w040
+c11s c21s x030 x031 c31s c40s c41s x040 x041 c50v c51s c60s c61s c70s c71s
 """
 
 
@@ -59,97 +56,83 @@ def tile_product_key_credit_s11_kernel(
         ca = keep.tile([P, 12], F32, name="ca")
         kaw = keep.tile([P, 2, 2048], U8, name="kaw", align_bytes=64)
         kas = keep.tile([P, 2, 1024], U8, name="kas", align_bytes=64)
-        kbc = keep.tile([P, 2, 1024], U32, name="kbc", align_bytes=64)
-        kbs = keep.tile([P, 2, 1024], U8, name="kbs", align_bytes=64)
-        pac = keep.tile([P, GROUPS, E], U32, name="pac", align_bytes=64)
-        pas = keep.tile([P, GROUPS, E], U8, name="pas", align_bytes=64)
+        kbc = keep.tile([P, 2, 2, 512], U32, name="kbc", align_bytes=64)
+        kbs = keep.tile([P, 2, 2, 512], U8, name="kbs", align_bytes=64)
+        pac = keep.tile([P, GROUPS, 512], U32, name="pac", align_bytes=64)
+        pas = keep.tile([P, GROUPS, 512], U8, name="pas", align_bytes=64)
+        pak = keep.tile([P, 4, GROUPS, P], U32, name="pak", align_bytes=64)
+        pal = keep.tile([P, 4, GROUPS, P], U8, name="pal", align_bytes=64)
         pbc = keep.tile([P, GROUPS, E], U32, name="pbc", align_bytes=64)
         pbs = keep.tile([P, GROUPS, E], U8, name="pbs", align_bytes=64)
-        qac = [keep.tile([P, 4, 2, P], U32, name="qac%d" % g, align_bytes=64) for g in range(GROUPS)]
-        qas = [keep.tile([P, 4, 2, P], U8, name="qas%d" % g, align_bytes=64) for g in range(GROUPS)]
-        qbc = [keep.tile([P, 4, 2, P], U32, name="qbc%d" % g, align_bytes=64) for g in range(GROUPS)]
-        qbs = [keep.tile([P, 4, 2, P], U8, name="qbs%d" % g, align_bytes=64) for g in range(GROUPS)]
+        qc = {
+            (s, g): keep.tile([P, 4, 2, P], U32, name="qc%d%d" % (s, g), align_bytes=64)
+            for s in range(2)
+            for g in range(GROUPS)
+        }
+        qs = {
+            (s, g): keep.tile([P, 4, 2, P], U8, name="qs%d%d" % (s, g), align_bytes=64)
+            for s in range(2)
+            for g in range(GROUPS)
+        }
         qbb = [keep.tile([P, 4, D], U8, name="qbb%d" % g, align_bytes=64) for g in range(GROUPS)]
         kbr = {
-            (g, h): keep.tile([P, 4, 512], BF16, name="kbr%d%d" % (g, h), align_bytes=64)
+            (c, h): keep.tile([P, 4, 512], BF16, name="kbr%d%d" % (c, h), align_bytes=64)
             for h in range(2)
-            for g in range(2)
+            for c in range(2)
         }
-
-        nc.vector.memset(warm[:], 0.0)
-        nc.vector.memset(crows[:], 0.0)
-        nc.vector.memset(srows[:], 0.0)
-        nc.vector.memset(kas[:].rearrange("p g n -> p (g n)").bitcast(I32), 0)
         make_identity(nc, ident[:])
-        nc.scalar.dma_start(
-            out=crows[0:6, :].bitcast(BF16), in_=coef.rearrange("s (g m) -> (s g) m", m=512)
-        )
-        nc.sync.dma_start(out=srows[0:8, :], in_=query_b_scale.rearrange("o (m n) -> (o m) n", n=P))
+
+        def bank(tag, name):
+            return psum.tile([P, 512], F32, name=name, tag=tag, bufs={"tp": 3, "mm": 5}[tag])
 
         qa_view = query_a.rearrange("(g p t) d -> g p t d", p=P, t=4)
         qb_view = query_b_bytes.rearrange("(g p t) d -> g p t d", p=P, t=4)
+        kb_view = keys_b.rearrange("(c p t) n -> c p t n", p=P, t=4)
         qar = {}
 
-        def load_qa(g, t):
-            qar[g, t] = work.tile([P, D], BF16, name="qar", tag="qar", bufs=12, align_bytes=64)
-            nc.sync.dma_start(out=qar[g, t][:], in_=qa_view[g][:, t, :])
+        def load(u):
+            a = [int(x) for x in u[1:] if x in "0123456789"]
+            q = nc.scalar if u[-1] == "A" else nc.sync
+            if u[0] == "a":
+                g, pair = a
+                qar[g, pair] = work.tile([P, 2, D], BF16, name="qar", tag="qar", bufs=5, align_bytes=64)
+                q.dma_start(out=qar[g, pair][:], in_=qa_view[g][:, 2 * pair : 2 * pair + 2, :])
+            elif u[0] == "b":
+                q.dma_start(out=qbb[a[0]][:], in_=qb_view[a[0]])
+            elif u[0] == "k":
+                c, h = a
+                q.dma_start(out=kbr[c, h][:], in_=kb_view[c][:, :, 512 * h : 512 * h + 512])
+            elif u[0] == "w":
+                q.dma_start(out=kaw[:], in_=keys_a_words.rearrange("g p x -> p g x"))
+            else:
+                for r in range(4):
+                    q.dma_start(
+                        out=kas[32 * r : 32 * r + 4, :, :].bitcast(I32),
+                        in_=keys_a_scales[:, 4 * r : 4 * r + 4, :].rearrange("g r n -> r g n").bitcast(I32),
+                    )
 
-        def load_qb(g):
-            nc.sync.dma_start(out=qbb[g][:], in_=qb_view[g])
-
-        kb_view = keys_b.rearrange("(g p t) n -> g p t n", p=P, t=4)
-
-        def load_ka():
-            nc.sync.dma_start(out=kaw[:], in_=keys_a_words.rearrange("g p x -> p g x"))
-
-        def load_kas():
-            for q in range(4):
-                nc.sync.dma_start(
-                    out=kas[32 * q : 32 * q + 4, :, :].bitcast(I32),
-                    in_=keys_a_scales[:, 4 * q : 4 * q + 4, :].rearrange("g r n -> r g n").bitcast(I32),
-                )
-
-        def load_kb(g, h):
-            nc.sync.dma_start(out=kbr[g, h][:], in_=kb_view[g][:, :, 512 * h : 512 * h + 512])
-
-        load_kb(0, 0)
-        load_qa(0, 0)
-        load_kas()
-        load_qa(0, 1)
-        load_qb(0)
-        load_qa(0, 2)
-        load_qa(0, 3)
-        load_qa(1, 0)
-        load_qa(1, 1)
-        load_qa(1, 2)
-        load_ka()
-        load_qb(1)
-        load_qa(1, 3)
-        load_kb(1, 0)
-        load_qa(2, 0)
-        load_qa(2, 1)
-        load_kb(0, 1)
-        load_qa(2, 2)
-        load_kb(1, 1)
-        load_qb(2)
-        load_qa(2, 3)
-
-        def bank(tag, bufs, name):
-            return psum.tile([P, 512], F32, name=name, tag=tag, bufs=bufs)
-
-        TP, MM = 3, 5
-        wbank = bank("mm", MM, "wbank")
+        wbank = bank("mm", "wbank")
 
         def warm_up():
             nc.tensor.matmul(wbank[:], lhsT=warm[:, 0:P], rhs=warm[:], start=True, stop=True)
 
         def head():
+            nc.vector.memset(crows[:], 0.0)
+            nc.vector.memset(srows[:], 0.0)
+            nc.vector.memset(warm[:], 0.0)
+            nc.vector.memset(kas[:].rearrange("p g n -> p (g n)").bitcast(I32), 0)
+            coef_rows = coef.rearrange("s (g m) -> (s g) m", m=512)
+            nc.scalar.dma_start(out=crows[0:4, :].bitcast(BF16), in_=coef_rows[0:4, :])
+            nc.scalar.dma_start(out=crows[4:6, :].bitcast(BF16), in_=coef_rows[4:6, :])
+            nc.sync.dma_start(out=srows[0:8, :], in_=query_b_scale.rearrange("o (m n) -> (o m) n", n=P))
+            for u in LOADS.split():
+                load(u)
             for i in range(4):
                 warm_up()
-            b0 = bank("tp", TP, "b0")
+            b0 = bank("tp", "b0")
+            nc.tensor.transpose(b0[:, 2 * P : 3 * P], srows[:], ident[:])
             for u in range(2):
                 nc.tensor.transpose(b0[:, P * u : P * u + P], crows[:, u::2], ident[:])
-            nc.tensor.transpose(b0[:, 2 * P : 3 * P], srows[:], ident[:])
             nc.vector.tensor_copy(out=scol[:], in_=b0[:, 2 * P : 2 * P + 8])
             nc.vector.tensor_copy(
                 out=coef_f[:].rearrange("p (x u e) -> p u x e", x=6, u=2),
@@ -157,7 +140,7 @@ def tile_product_key_credit_s11_kernel(
             )
             banks = []
             for half in range(2):
-                bb = bank("tp", TP, "bb")
+                bb = bank("tp", "bb")
                 for j in range(4):
                     m = 4 * half + j
                     nc.tensor.transpose(
@@ -178,145 +161,157 @@ def tile_product_key_credit_s11_kernel(
             nc.gpsimd.tensor_tensor(out=gt[:], in0=gt[:], in1=lt[:], op=ALU.subtract)
             nc.gpsimd.tensor_tensor(out=ca[:], in0=coef_f[:, 0:12], in1=gt[:], op=ALU.mult)
 
-        prod = {}
+        def move(engine, dst, src):
+            if engine == "s":
+                nc.scalar.copy(out=dst, in_=src)
+            else:
+                nc.vector.tensor_copy(out=dst, in_=src)
+
+        prod, grp, kbg, ex, pg = {}, {}, {}, {}, {}
 
         def product(g, t):
-            w = work.tile([P, D], BF16, name="prod", tag="prod", bufs=6, align_bytes=64)
+            w = work.tile([P, D], BF16, name="prod", tag="prod", bufs=4, align_bytes=64)
             nc.vector.tensor_tensor(out=w[:], in0=qbb[g][:, t, :].bitcast(FP8), in1=sbc[:], op=ALU.mult)
             prod[g, t] = w
 
-        grp = {}
-
         def turn(side, g, t, engine):
-            src = qar[g, t][:] if side == 0 else prod[g, t][:]
+            src = qar[g, t // 2][:, t % 2, :] if side == 0 else prod[g, t][:]
             words = src.bitcast(F32)
-            b = bank("tp", TP, "tb")
+            b = bank("tp", "tb")
             for c in range(2):
                 for u in range(2):
                     j = 2 * c + u
                     nc.tensor.transpose(
                         b[:, P * j : P * j + P], words[:, 256 * c + u : 256 * c + 256 : 2], ident[:]
                     )
-            if (side, g, t // 2) not in grp:
-                grp[side, g, t // 2] = work.tile(
-                    [P, 2, 2, P, 2], F32, name="grp", tag="grp", bufs=4, align_bytes=64
-                )
-            dst = grp[side, g, t // 2][:, t % 2, :, :, :]
-            srcb = b[:].rearrange("p (c u r) -> p c r u", c=2, u=2)
-            if engine == "s":
-                nc.scalar.copy(out=dst, in_=srcb)
-            else:
-                nc.vector.tensor_copy(out=dst, in_=srcb)
+            if (side, g) not in grp:
+                grp[side, g] = work.tile([P, 4, 2, P, 2], F32, name="grp", tag="grp", bufs=3, align_bytes=64)
+            move(engine, grp[side, g][:, t, :, :, :], b[:].rearrange("p (c u r) -> p c r u", c=2, u=2))
 
-        def quant_q(side, g, pair):
-            codes, scales = (qac[g], qas[g]) if side == 0 else (qbc[g], qbs[g])
+        def quant_q(side, g):
             nc.vector.quantize_mx(
-                out=codes[:, 2 * pair : 2 * pair + 2, :, :].rearrange("p a c r -> p (a c r)").bitcast(E4M3X4),
-                scales=scales[:, 2 * pair : 2 * pair + 2, :, :].rearrange("p a c r -> p (a c r)"),
-                in_=grp[side, g, pair][:].rearrange("p a c r u -> p (a c r u)").bitcast(BF16),
+                out=qc[side, g][:].rearrange("p a c r -> p (a c r)").bitcast(E4M3X4),
+                scales=qs[side, g][:].rearrange("p a c r -> p (a c r)"),
+                in_=grp[side, g][:].rearrange("p a c r u -> p (a c r u)").bitcast(BF16),
             )
-
-        kbg = {}
 
         def kb_inter(c, h, engine):
-            w = work.tile([P, 512, 4], BF16, name="kbg", tag="kbg", bufs=2, align_bytes=64)
-            dst = w[:].rearrange("p (c i) t -> p c t i", i=4)
-            src = kbr[c, h][:].rearrange("p t (c i) -> p c t i", i=4)
-            if engine == "s":
-                nc.scalar.copy(out=dst, in_=src)
-            else:
-                nc.vector.tensor_copy(out=dst, in_=src)
-            kbg[c, h] = w
-
-        def kb_quant(c, h):
-            nc.vector.quantize_mx(
-                out=kbc[:, c, 512 * h : 512 * h + 512].bitcast(E4M3X4),
-                scales=kbs[:, c, 512 * h : 512 * h + 512],
-                in_=kbg[c, h][:].rearrange("p n t -> p (n t)"),
+            if h not in kbg:
+                kbg[h] = work.tile([P, 2, 512, 4], BF16, name="kbg", tag="kbg", bufs=1, align_bytes=64)
+            move(
+                engine,
+                kbg[h][:, c, :, :].rearrange("p (c i) t -> p c t i", i=4),
+                kbr[c, h][:].rearrange("p t (c i) -> p c t i", i=4),
             )
 
-        ea, eb = {}, {}
+        def kb_quant(h):
+            nc.vector.quantize_mx(
+                out=kbc[:, h, :, :].rearrange("p c n -> p (c n)").bitcast(E4M3X4),
+                scales=kbs[:, h, :, :].rearrange("p c n -> p (c n)"),
+                in_=kbg[h][:].rearrange("p c n t -> p (c n t)"),
+            )
 
-        def score(side, bi, g, t):
-            s0, w = BLOCKS[side][bi]
-            b = bank("mm", MM, "sc")
-            codes, scales = (qac, qas) if side == 0 else (qbc, qbs)
+        def scores(dst, side, g, t, s0, w):
             for c in range(2):
                 if side == 0:
                     rhs = kaw[:, c, 2 * s0 : 2 * s0 + 2 * w].bitcast(E2M1X4)
                     rsc = kas[:, c, s0 : s0 + w]
                 else:
-                    rhs = kbc[:, c, s0 : s0 + w].bitcast(E4M3X4)
-                    rsc = kbs[:, c, s0 : s0 + w]
+                    rhs = kbc[:, s0 // 512, c, :].bitcast(E4M3X4)
+                    rsc = kbs[:, s0 // 512, c, :]
                 nc.tensor.matmul_mx(
-                    out=b[:, 0:w],
-                    lhsT=codes[g][:, t, c, :].bitcast(E4M3X4),
-                    lhsT_scale=scales[g][:, t, c, :],
+                    out=dst,
+                    lhsT=qc[side, g][:, t, c, :].bitcast(E4M3X4),
+                    lhsT_scale=qs[side, g][:, t, c, :],
                     rhs=rhs,
                     rhs_scale=rsc,
                     start=(c == 0),
                     stop=(c == 1),
                 )
-            store = ea if side == 0 else eb
-            if (bi, g) not in store:
-                if side == 0:
-                    store[bi, g] = work.tile([P, 4, w], F32, name="ea", tag="ea", bufs=3)
-                else:
-                    store[bi, g] = work.tile([P, 4, w], BF16, name="eb", tag="eb", bufs=3)
-            k = 4 * g + t
-            if side == 0:
-                nc.scalar.activation(out=store[bi, g][:, t, :], in_=b[:, 0:w], func=ACT.Exp)
-            else:
-                nc.scalar.activation(
-                    out=store[bi, g][:, t, :], in_=b[:, 0:w], func=ACT.Exp, bias=lnb[:, k : k + 1]
-                )
 
-        pg = {}
+        def score(side, bi, g, t):
+            b = bank("mm", "sc")
+            k = 4 * g + t
+            if side == 0 and bi > 0:
+                for j in range(4):
+                    scores(b[:, P * j : P * j + P], 0, g, j, 384 + P * bi, P)
+                if bi not in ex:
+                    ex[bi] = work.tile([P, GROUPS, P, 4], F32, name="ea", tag="ea", bufs=3, align_bytes=64)
+                nc.scalar.activation(
+                    out=ex[bi][:, g, :, :], in_=b[:].rearrange("p (t n) -> p n t", t=4), func=ACT.Exp
+                )
+                return
+            scores(b[:], side, g, t, 512 * bi, 512)
+            if (side, bi, g) not in ex:
+                ex[side, bi, g] = work.tile(
+                    [P, 4, 512], BF16 if side else F32, name="ex", tag="eb" if side else "ea", bufs=3, align_bytes=64
+                )
+            dst = ex[side, bi, g][:, t, :]
+            if side == 0:
+                nc.scalar.activation(out=dst, in_=b[:], func=ACT.Exp)
+            else:
+                nc.scalar.activation(out=dst, in_=b[:], func=ACT.Exp, bias=lnb[:, k : k + 1])
 
         def weigh(side, bi, g):
-            w = BLOCKS[side][bi][1]
-            o = work.tile([P, w, 4], BF16, name="pg", tag="pg", bufs=4, align_bytes=64)
-            e = (ea if side == 0 else eb)[bi, g][:].rearrange("p t (c i) -> p c t i", i=4)
+            if side == 0 and bi > 0:
+                o = work.tile([P, GROUPS, P, 4], BF16, name="pg", tag="pg", bufs=4, align_bytes=64)
+                nc.vector.tensor_tensor(
+                    out=o[:],
+                    in0=ex[bi][:],
+                    in1=ca[:]
+                    .rearrange("p (g t) -> p g t", t=4)
+                    .unsqueeze(2)
+                    .to_broadcast([P, GROUPS, P, 4]),
+                    op=ALU.mult,
+                )
+                pg[side, bi] = o
+                return
+            o = work.tile([P, 512, 4], BF16, name="pg", tag="pg", bufs=4, align_bytes=64)
+            src = ex[side, bi, g][:].rearrange("p t (c i) -> p c t i", i=4)
             dst = o[:].rearrange("p (c i) t -> p c t i", i=4)
             if side == 0:
                 nc.vector.tensor_tensor(
                     out=dst,
-                    in0=e,
-                    in1=ca[:, 4 * g : 4 * g + 4].unsqueeze(1).unsqueeze(3).to_broadcast([P, w // 4, 4, 4]),
+                    in0=src,
+                    in1=ca[:, 4 * g : 4 * g + 4].unsqueeze(1).unsqueeze(3).to_broadcast([P, 128, 4, 4]),
                     op=ALU.mult,
                 )
             else:
-                nc.vector.tensor_copy(out=dst, in_=e)
+                nc.vector.tensor_copy(out=dst, in_=src)
             pg[side, bi, g] = o
 
-        def quant_p(side, bi, g):
-            s0, w = BLOCKS[side][bi]
-            codes, scales = (pac, pas) if side == 0 else (pbc, pbs)
-            nc.vector.quantize_mx(
-                out=codes[:, g, s0 : s0 + w].bitcast(E4M3X4),
-                scales=scales[:, g, s0 : s0 + w],
-                in_=pg[side, bi, g][:].rearrange("p n t -> p (n t)"),
-            )
+        def quant_p(side, bi, z):
+            if side == 0 and bi > 0:
+                lo, n = (0, 2) if z == 0 else (2, 1)
+                codes = pak[:, bi - 1, lo : lo + n, :].rearrange("p g n -> p (g n)")
+                scales = pal[:, bi - 1, lo : lo + n, :].rearrange("p g n -> p (g n)")
+                src = pg[side, bi][:, lo : lo + n, :, :].rearrange("p g n t -> p (g n t)")
+            else:
+                s0 = 512 * bi
+                codes = pbc[:, z, s0 : s0 + 512] if side else pac[:, z, :]
+                scales = pbs[:, z, s0 : s0 + 512] if side else pas[:, z, :]
+                src = pg[side, bi, z][:].rearrange("p n t -> p (n t)")
+            nc.vector.quantize_mx(out=codes.bitcast(E4M3X4), scales=scales, in_=src)
 
         def credit(i, bi, engine):
-            s0, w = BLOCKS[1][bi]
-            b = bank("mm", MM, "cr")
+            b = bank("mm", "cr")
             for g in range(GROUPS):
+                if i < 4:
+                    lhsT, lsc = pac[:, g, P * i : P * i + P], pas[:, g, P * i : P * i + P]
+                else:
+                    lhsT, lsc = pak[:, i - 4, g, :], pal[:, i - 4, g, :]
                 nc.tensor.matmul_mx(
-                    out=b[:, 0:w],
-                    lhsT=pac[:, g, P * i : P * i + P].bitcast(E4M3X4),
-                    lhsT_scale=pas[:, g, P * i : P * i + P],
-                    rhs=pbc[:, g, s0 : s0 + w].bitcast(E4M3X4),
-                    rhs_scale=pbs[:, g, s0 : s0 + w],
+                    out=b[:],
+                    lhsT=lhsT.bitcast(E4M3X4),
+                    lhsT_scale=lsc,
+                    rhs=pbc[:, g, 512 * bi : 512 * bi + 512].bitcast(E4M3X4),
+                    rhs_scale=pbs[:, g, 512 * bi : 512 * bi + 512],
                     start=(g == 0),
                     stop=(g == GROUPS - 1),
                 )
-            o = work.tile([P, w], F32, name="o", tag="o", bufs=4)
-            if engine == "s":
-                nc.scalar.copy(out=o[:], in_=b[:, 0:w])
-            else:
-                nc.vector.tensor_copy(out=o[:], in_=b[:, 0:w])
-            nc.sync.dma_start(out=out[P * i : P * i + P, s0 : s0 + w], in_=o[:])
+            o = work.tile([P, 512], F32, name="o", tag="o", bufs=4)
+            move(engine, o[:], b[:])
+            nc.sync.dma_start(out=out[P * i : P * i + P, 512 * bi : 512 * bi + 512], in_=o[:])
 
         def emit(u):
             k = u[0]
@@ -327,7 +322,7 @@ def tile_product_key_credit_s11_kernel(
             elif k == "t":
                 turn(a[0], a[1], a[2], e)
             elif k == "q":
-                quant_q(*a)
+                quant_q(a[0], a[1])
             elif k == "i":
                 kb_inter(a[0], a[1], e)
             elif k == "j":

@@ -19,16 +19,17 @@ E2M1X4 = mybir.dt.float4_e2m1fn_x4
 ACT = mybir.ActivationFunctionType
 ALU = mybir.AluOpType
 
-LOADS = "a00A k00 b0 k10 a01 b1 a10 a11 a20 k01 x b2 w a21 k11A"
+LOADS = "a00 x a01 b0 k00 a10 w k10 b1 b2 a11 a20A a21 k01A k11"
 ORDER = """
-t000v t001v i00s p00 i10s t100s t002s p01 p02 t101s t003s t010s t102s p03 t011s p10 t103s p11 t012s
-p12 q000 t110s p13 t013s q100 t111s j0 p20 q010 t112s t020s p21 t021s t113s s0000 s1000 p22 p23
-s1001 s0001 s0002 i01v s1002 s0003 s1003 s0010 t120s t022s t023s q110 i11v w100 t121s q020 t122s
-t123s s0011 q120 s1010 s1011 s0012 s0013 s1012 s0020 s1013 w000 s1020 s1021 s1022 s0021 s0022 j1
-s1023 x100 s0023 s0100 w101 s1100 s0110 s1101 x000 w001 s1102 w102 w002 s1103 s0120 x101 s0200 s1110
-x001 s1111 s0210 s1112 s1113 s1120 w110 s1121 s0220 s1122 x002 x102 w111 s1123 s0300 w010 s0310 x110
-c00s c10s s0320 s0400 w112 c20s x111 c30s s0410 x112 s0420 x010 c01s w020 x011 w030 x020 x021 w040
-c11s c21s x030 x031 c31s c40s c41s x040 x041 c50v c51s c60s c61s c70s c71s
+p00 p01 d d p02 d d d d d t000s t001s t002s d p03 d d t003s t100s t101s d d q000 i00s d t102s i10v
+p10 p11 t103s s0000 s0001 p12 t010s t110s q100 t011s s0002 t012s p13 t111s t112s j0 s0003 p20 t013s
+t020s t113s s1000 p21 p22 t021s q010 t022s t023s p23 q110 s1001 i01v d d s1002 i11v t120s t121s
+t122s t123s s1003 s0010 s0011 q120 s1010 s0012 s1011 q020 s1012 w100 s1013 j1 s0013 w000 s0020 s1020
+s0021 s0022 s1021 w101 s1022 s1023 x100 s1100 s1101 w001 s1102 s0023 x000 s1103 w102 s1110 s1111
+s1112 w002 s0100 x101 s0110 s1113 s0120 s0200 s1120 x001 s0210 s1121 s1122 s1123 s0220 x102 x002 d
+s0300 w110 s0310 w111 c00s c10s x110 c20s s0320 c30s w112 x111 x112 w010 w020 s0400 s0410 c01s c11s
+x010 s0420 x011 c21s c31s c40s x020 c41s x021 c50s w030 x030 c51s x031 c60s w040 x040 x041 c61v c70v
+c71s d d
 """
 
 
@@ -111,10 +112,9 @@ def tile_product_key_credit_s11_kernel(
                         in_=keys_a_scales[:, 4 * r : 4 * r + 4, :].rearrange("g r n -> r g n").bitcast(I32),
                     )
 
-        wbank = bank("mm", "wbank")
-
         def warm_up():
-            nc.tensor.matmul(wbank[:], lhsT=warm[:, 0:P], rhs=warm[:], start=True, stop=True)
+            w = bank("mm", "wbank")
+            nc.tensor.matmul(w[:], lhsT=warm[:, 0:P], rhs=warm[:], start=True, stop=True)
 
         def head():
             nc.vector.memset(crows[:], 0.0)
@@ -127,7 +127,7 @@ def tile_product_key_credit_s11_kernel(
             nc.sync.dma_start(out=srows[0:8, :], in_=query_b_scale.rearrange("o (m n) -> (o m) n", n=P))
             for u in LOADS.split():
                 load(u)
-            for i in range(4):
+            for i in range(0):
                 warm_up()
             b0 = bank("tp", "b0")
             nc.tensor.transpose(b0[:, 2 * P : 3 * P], srows[:], ident[:])
@@ -317,7 +317,9 @@ def tile_product_key_credit_s11_kernel(
             k = u[0]
             a = [int(x) for x in u[1:] if x in "0123456789"]
             e = u[-1]
-            if k == "p":
+            if k == "d":
+                warm_up()
+            elif k == "p":
                 product(*a)
             elif k == "t":
                 turn(a[0], a[1], a[2], e)
@@ -338,11 +340,5 @@ def tile_product_key_credit_s11_kernel(
 
         with tc.manual_schedule():
             head()
-            turns, scored = 0, False
             for u in ORDER.split():
                 emit(u)
-                scored = scored or u[0] == "s"
-                if u[0] == "t" and not scored:
-                    turns += 1
-                    if turns % 2 == 0:
-                        warm_up()

@@ -5,7 +5,10 @@ from concourse.masks import make_identity
 
 T, D, E = 1536, 1024, 1024
 P = 128
-GROUPS = 3
+SLOTS = 4
+GROUPS = T // (P * SLOTS)
+PASSES = D // (P * SLOTS)
+HALF = 512
 FLOPS = 3 * 2 * T * D * E
 
 F32 = mybir.dt.float32
@@ -19,17 +22,20 @@ E2M1X4 = mybir.dt.float4_e2m1fn_x4
 ACT = mybir.ActivationFunctionType
 ALU = mybir.AluOpType
 
-LOADS = "a00 x a01 b0 k00 a10 w k10 b1 b2 a11 a20A a21 k01A k11"
+BANKS = {"turn": 4, "mm": 4}
+
+LOADS = "k00A k10A a00A a01A b0 a10 w a11 x b1 k01 k11 a20 a21 b2"
+
 ORDER = """
-p00 p01 d d p02 d d d d d t000s t001s t002s d p03 d d t003s t100s t101s d d q000 i00s d t102s i10v
-p10 p11 t103s s0000 s0001 p12 t010s t110s q100 t011s s0002 t012s p13 t111s t112s j0 s0003 p20 t013s
-t020s t113s s1000 p21 p22 t021s q010 t022s t023s p23 q110 s1001 i01v d d s1002 i11v t120s t121s
-t122s t123s s1003 s0010 s0011 q120 s1010 s0012 s1011 q020 s1012 w100 s1013 j1 s0013 w000 s0020 s1020
-s0021 s0022 s1021 w101 s1022 s1023 x100 s1100 s1101 w001 s1102 s0023 x000 s1103 w102 s1110 s1111
-s1112 w002 s0100 x101 s0110 s1113 s0120 s0200 s1120 x001 s0210 s1121 s1122 s1123 s0220 x102 x002 d
-s0300 w110 s0310 w111 c00s c10s x110 c20s s0320 c30s w112 x111 x112 w010 w020 s0400 s0410 c01s c11s
-x010 s0420 x011 c21s c31s c40s x020 c41s x021 c50s w030 x030 c51s x031 c60s w040 x040 x041 c61v c70v
-c71s d d
+h1 d i00s i10v d d j0 h2s t000s d d d t001s p00 t002s t003s p01 p02 d d h3 t100s q00 p03 t010s d d
+p10 t101s p11 t011s s0000 i01v t102s t103s q10 t012s s0001 s0002 t013s p12 t110s t111s s0003 s1000
+p13 s1001 p20 s1002 p21 s1003 q01 t112s t113s t020s t021s t120s s0010 p22 s0011 i11v p23 t121s q11
+w100 t122s t022s t023s q02 t123s q12 s0012 s0013 j1 s1010 s1011 s1012 s1013 x100 s0020 w000 w001
+s0021 x000 s1020 x001 s0022 s1021 s1022 s0023 s1023 s0100 w101 s1100 w102 s1101 s1102 s1103 w002
+w110 s0110 s0120 s0200 s1110 s1111 s1112 x101 x102 s1113 s0210 s1120 s1121 s0220 x002 s0300 w010
+s1122 w111 s0310 s1123 s0320 w112 x110 x111 s0400 c00s x112 c10s w020 x010 c20s s0410 x011 c30s
+s0420 c01s c11s c21s x020 w030 c31s x021 c40s c41s x030 x031 w040 x040 c50s x041 c51s c60v c61s c70s
+c71v
 """
 
 
@@ -43,302 +49,319 @@ def tile_product_key_credit_s11_kernel(
         psum = ctx.enter_context(tc.psum_pool(name="psum", bufs=1))
 
         ident = keep.tile([P, P], F32, name="ident")
-        srows = keep.tile([P, P], F32, name="srows")
-        scol = keep.tile([P, 8], F32, name="scol")
-        sbc = keep.tile([P, D], F32, name="sbc", align_bytes=64)
-        crows = keep.tile([P, 2 * P], F32, name="crows")
-        warm = keep.tile([P, 512], BF16, name="warm")
-        junk = keep.tile([P, 1], F32, name="junk")
-        coef_f = keep.tile([P, 24], F32, name="coef_f")
-        gt = keep.tile([P, 12], F32, name="gt")
-        lt = keep.tile([P, 12], F32, name="lt")
-        lnb = keep.tile([P, 12], F32, name="lnb")
-        mag = keep.tile([P, 12], F32, name="mag")
-        ca = keep.tile([P, 12], F32, name="ca")
-        kaw = keep.tile([P, 2, 2048], U8, name="kaw", align_bytes=64)
-        kas = keep.tile([P, 2, 1024], U8, name="kas", align_bytes=64)
-        kbc = keep.tile([P, 2, 2, 512], U32, name="kbc", align_bytes=64)
-        kbs = keep.tile([P, 2, 2, 512], U8, name="kbs", align_bytes=64)
-        pac = keep.tile([P, GROUPS, 512], U32, name="pac", align_bytes=64)
-        pas = keep.tile([P, GROUPS, 512], U8, name="pas", align_bytes=64)
-        pak = keep.tile([P, 4, GROUPS, P], U32, name="pak", align_bytes=64)
-        pal = keep.tile([P, 4, GROUPS, P], U8, name="pal", align_bytes=64)
-        pbc = keep.tile([P, GROUPS, E], U32, name="pbc", align_bytes=64)
-        pbs = keep.tile([P, GROUPS, E], U8, name="pbs", align_bytes=64)
-        qc = {
-            (s, g): keep.tile([P, 4, 2, P], U32, name="qc%d%d" % (s, g), align_bytes=64)
-            for s in range(2)
-            for g in range(GROUPS)
-        }
-        qs = {
-            (s, g): keep.tile([P, 4, 2, P], U8, name="qs%d%d" % (s, g), align_bytes=64)
-            for s in range(2)
-            for g in range(GROUPS)
-        }
-        qbb = [keep.tile([P, 4, D], U8, name="qbb%d" % g, align_bytes=64) for g in range(GROUPS)]
-        kbr = {
-            (c, h): keep.tile([P, 4, 512], BF16, name="kbr%d%d" % (c, h), align_bytes=64)
-            for h in range(2)
-            for c in range(2)
-        }
+        dummy = keep.tile([P, HALF], BF16, name="dummy")
+        coef_rows = keep.tile([P, HALF // 2], F32, name="coef_rows")
+        scale_rows = keep.tile([P, P], F32, name="scale_rows")
+        scale_cols = keep.tile([P, D // P], F32, name="scale_cols")
+        scale_all = keep.tile([P, D], F32, name="scale_all", align_bytes=64)
+        coefs = keep.tile([P, 2 * GROUPS * SLOTS], F32, name="coefs")
+        coef_b_abs = keep.tile([P, GROUPS * SLOTS], F32, name="coef_b_abs")
+        coef_b_ln = keep.tile([P, GROUPS * SLOTS], F32, name="coef_b_ln")
+        coef_b_sign = keep.tile([P, GROUPS * SLOTS], F32, name="coef_b_sign")
+        negative = keep.tile([P, GROUPS * SLOTS], F32, name="negative")
+        factor_a = keep.tile([P, GROUPS * SLOTS], F32, name="factor_a")
+        unused = keep.tile([P, 1], F32, name="unused")
+
+        ka_words = keep.tile([P, PASSES, 2 * E], U8, name="ka_words", align_bytes=64)
+        ka_scales = keep.tile([P, PASSES, E], U8, name="ka_scales", align_bytes=64)
+        kb_codes = keep.tile([P, 2, PASSES, HALF], U32, name="kb_codes", align_bytes=64)
+        kb_scales = keep.tile([P, 2, PASSES, HALF], U8, name="kb_scales", align_bytes=64)
+        pa_codes = keep.tile([P, GROUPS, HALF], U32, name="pa_codes", align_bytes=64)
+        pa_scales = keep.tile([P, GROUPS, HALF], U8, name="pa_scales", align_bytes=64)
+        pa_blk_codes = keep.tile([P, HALF // P, GROUPS, P], U32, name="pa_blk_codes", align_bytes=64)
+        pa_blk_scales = keep.tile([P, HALF // P, GROUPS, P], U8, name="pa_blk_scales", align_bytes=64)
+        pb_codes = keep.tile([P, GROUPS, E], U32, name="pb_codes", align_bytes=64)
+        pb_scales = keep.tile([P, GROUPS, E], U8, name="pb_scales", align_bytes=64)
+        q_codes, q_scales = {}, {}
+        for side in range(2):
+            for g in range(GROUPS):
+                q_codes[side, g] = keep.tile([P, SLOTS, PASSES, P], U32, name="qc%d%d" % (side, g), align_bytes=64)
+                q_scales[side, g] = keep.tile([P, SLOTS, PASSES, P], U8, name="qs%d%d" % (side, g), align_bytes=64)
+        qb_bytes = [keep.tile([P, SLOTS, D], U8, name="qb_bytes%d" % g, align_bytes=64) for g in range(GROUPS)]
+        kb_raw = {}
+        for half in range(2):
+            for c in range(PASSES):
+                kb_raw[c, half] = keep.tile([P, SLOTS, HALF], BF16, name="kb_raw%d%d" % (c, half), align_bytes=64)
+
         make_identity(nc, ident[:])
 
-        def bank(tag, name):
-            return psum.tile([P, 512], F32, name=name, tag=tag, bufs={"tp": 3, "mm": 5}[tag])
+        def bank(use, name):
+            return psum.tile([P, HALF], F32, name=name, tag=use, bufs=BANKS[use])
 
-        qa_view = query_a.rearrange("(g p t) d -> g p t d", p=P, t=4)
-        qb_view = query_b_bytes.rearrange("(g p t) d -> g p t d", p=P, t=4)
-        kb_view = keys_b.rearrange("(c p t) n -> c p t n", p=P, t=4)
-        qar = {}
-
-        def load(u):
-            a = [int(x) for x in u[1:] if x in "0123456789"]
-            q = nc.scalar if u[-1] == "A" else nc.sync
-            if u[0] == "a":
-                g, pair = a
-                qar[g, pair] = work.tile([P, 2, D], BF16, name="qar", tag="qar", bufs=5, align_bytes=64)
-                q.dma_start(out=qar[g, pair][:], in_=qa_view[g][:, 2 * pair : 2 * pair + 2, :])
-            elif u[0] == "b":
-                q.dma_start(out=qbb[a[0]][:], in_=qb_view[a[0]])
-            elif u[0] == "k":
-                c, h = a
-                q.dma_start(out=kbr[c, h][:], in_=kb_view[c][:, :, 512 * h : 512 * h + 512])
-            elif u[0] == "w":
-                q.dma_start(out=kaw[:], in_=keys_a_words.rearrange("g p x -> p g x"))
-            else:
-                for r in range(4):
-                    q.dma_start(
-                        out=kas[32 * r : 32 * r + 4, :, :].bitcast(I32),
-                        in_=keys_a_scales[:, 4 * r : 4 * r + 4, :].rearrange("g r n -> r g n").bitcast(I32),
-                    )
-
-        def warm_up():
-            w = bank("mm", "wbank")
-            nc.tensor.matmul(w[:], lhsT=warm[:, 0:P], rhs=warm[:], start=True, stop=True)
-
-        def head():
-            nc.vector.memset(crows[:], 0.0)
-            nc.vector.memset(srows[:], 0.0)
-            nc.vector.memset(warm[:], 0.0)
-            nc.vector.memset(kas[:].rearrange("p g n -> p (g n)").bitcast(I32), 0)
-            coef_rows = coef.rearrange("s (g m) -> (s g) m", m=512)
-            nc.scalar.dma_start(out=crows[0:4, :].bitcast(BF16), in_=coef_rows[0:4, :])
-            nc.scalar.dma_start(out=crows[4:6, :].bitcast(BF16), in_=coef_rows[4:6, :])
-            nc.sync.dma_start(out=srows[0:8, :], in_=query_b_scale.rearrange("o (m n) -> (o m) n", n=P))
-            for u in LOADS.split():
-                load(u)
-            for i in range(0):
-                warm_up()
-            b0 = bank("tp", "b0")
-            nc.tensor.transpose(b0[:, 2 * P : 3 * P], srows[:], ident[:])
-            for u in range(2):
-                nc.tensor.transpose(b0[:, P * u : P * u + P], crows[:, u::2], ident[:])
-            nc.vector.tensor_copy(out=scol[:], in_=b0[:, 2 * P : 2 * P + 8])
-            nc.vector.tensor_copy(
-                out=coef_f[:].rearrange("p (x u e) -> p u x e", x=6, u=2),
-                in_=b0[:, 0 : 2 * P].bitcast(BF16).rearrange("p (u r e) -> p u r e", u=2, e=2)[:, :, 0:6, :],
-            )
-            banks = []
-            for half in range(2):
-                bb = bank("tp", "bb")
-                for j in range(4):
-                    m = 4 * half + j
-                    nc.tensor.transpose(
-                        bb[:, P * j : P * j + P], scol[:, m : m + 1].to_broadcast([P, P]), ident[:]
-                    )
-                banks.append(bb)
-            cb = coef_f[:, 12:24]
-            nc.vector.scalar_tensor_tensor(
-                out=mag[:], in0=cb, scalar=-1.0, in1=cb, op0=ALU.mult, op1=ALU.max
-            )
-            nc.vector.tensor_copy(out=sbc[:, 0:512], in_=banks[0][:])
-            nc.vector.tensor_scalar(out=mag[:], in0=mag[:], scalar1=1e-19, scalar2=None, op0=ALU.max)
-            nc.scalar.activation(out=lnb[:], in_=mag[:], func=ACT.Ln)
-            nc.scalar.activation(out=junk[:], in_=lnb[:, 0:1], func=ACT.Exp)
-            nc.vector.tensor_copy(out=sbc[:, 512:1024], in_=banks[1][:])
-            nc.gpsimd.tensor_scalar(out=gt[:], in0=cb, scalar1=0.0, scalar2=None, op0=ALU.is_gt)
-            nc.gpsimd.tensor_scalar(out=lt[:], in0=cb, scalar1=0.0, scalar2=None, op0=ALU.is_lt)
-            nc.gpsimd.tensor_tensor(out=gt[:], in0=gt[:], in1=lt[:], op=ALU.subtract)
-            nc.gpsimd.tensor_tensor(out=ca[:], in0=coef_f[:, 0:12], in1=gt[:], op=ALU.mult)
-
-        def move(engine, dst, src):
+        def copy(engine, dst, src):
             if engine == "s":
                 nc.scalar.copy(out=dst, in_=src)
             else:
                 nc.vector.tensor_copy(out=dst, in_=src)
 
-        prod, grp, kbg, ex, pg = {}, {}, {}, {}, {}
+        qa_view = query_a.rearrange("(g p t) d -> g p t d", p=P, t=SLOTS)
+        qb_view = query_b_bytes.rearrange("(g p t) d -> g p t d", p=P, t=SLOTS)
+        kb_view = keys_b.rearrange("(c p t) n -> c p t n", p=P, t=SLOTS)
+        qa_raw = {}
 
-        def product(g, t):
-            w = work.tile([P, D], BF16, name="prod", tag="prod", bufs=4, align_bytes=64)
-            nc.vector.tensor_tensor(out=w[:], in0=qbb[g][:, t, :].bitcast(FP8), in1=sbc[:], op=ALU.mult)
-            prod[g, t] = w
+        def load(step):
+            n = [int(x) for x in step[1:] if x in "0123456789"]
+            queue = nc.scalar if step[-1] == "A" else nc.sync
+            if step[0] == "a":
+                g, pair = n
+                qa_raw[g, pair] = work.tile([P, 2, D], BF16, name="qa_raw", tag="qa_raw", bufs=5, align_bytes=64)
+                queue.dma_start(out=qa_raw[g, pair][:], in_=qa_view[g][:, 2 * pair : 2 * pair + 2, :])
+            elif step[0] == "b":
+                queue.dma_start(out=qb_bytes[n[0]][:], in_=qb_view[n[0]])
+            elif step[0] == "k":
+                c, half = n
+                queue.dma_start(out=kb_raw[c, half][:], in_=kb_view[c][:, :, HALF * half : HALF * half + HALF])
+            elif step[0] == "w":
+                queue.dma_start(out=ka_words[:], in_=keys_a_words.rearrange("c p x -> p c x"))
+            else:
+                for q in range(4):
+                    queue.dma_start(
+                        out=ka_scales[32 * q : 32 * q + 4, :, :].bitcast(I32),
+                        in_=keys_a_scales[:, 4 * q : 4 * q + 4, :].rearrange("c r n -> r c n").bitcast(I32),
+                    )
+
+        def first_loads():
+            nc.vector.memset(coef_rows[:], 0.0)
+            nc.vector.memset(scale_rows[:], 0.0)
+            nc.vector.memset(dummy[:], 0.0)
+            nc.vector.memset(ka_scales[:].rearrange("p c n -> p (c n)").bitcast(I32), 0)
+            rows = coef.rearrange("s (g m) -> (s g) m", m=HALF)
+            nc.scalar.dma_start(out=coef_rows[0:4, :].bitcast(BF16), in_=rows[0:4, :])
+            nc.scalar.dma_start(out=coef_rows[4:6, :].bitcast(BF16), in_=rows[4:6, :])
+            nc.sync.dma_start(out=scale_rows[0 : D // P, :], in_=query_b_scale.rearrange("o (r n) -> (o r) n", n=P))
+            for step in LOADS.split():
+                load(step)
+
+        def busy():
+            b = bank("mm", "busy")
+            nc.tensor.matmul(b[:], lhsT=dummy[:, 0:P], rhs=dummy[:], start=True, stop=True)
+
+        def head_columns():
+            b = bank("turn", "head")
+            nc.tensor.transpose(b[:, 2 * P : 3 * P], scale_rows[:], ident[:])
+            for u in range(2):
+                nc.tensor.transpose(b[:, P * u : P * u + P], coef_rows[:, u::2], ident[:])
+            nc.vector.tensor_copy(out=scale_cols[:], in_=b[:, 2 * P : 2 * P + D // P])
+            nc.vector.tensor_copy(
+                out=coefs[:].rearrange("p (x u e) -> p u x e", u=2, e=2),
+                in_=b[:, 0 : 2 * P].bitcast(BF16).rearrange("p (u r e) -> p u r e", u=2, e=2)[:, :, 0 : 2 * GROUPS, :],
+            )
+            coef_a = coefs[:, 0 : GROUPS * SLOTS]
+            coef_b = coefs[:, GROUPS * SLOTS : 2 * GROUPS * SLOTS]
+            nc.vector.scalar_tensor_tensor(
+                out=coef_b_abs[:], in0=coef_b, scalar=-1.0, in1=coef_b, op0=ALU.mult, op1=ALU.max
+            )
+            nc.vector.tensor_scalar(
+                out=coef_b_abs[:], in0=coef_b_abs[:], scalar1=1e-19, scalar2=None, op0=ALU.max
+            )
+            nc.gpsimd.tensor_scalar(out=coef_b_sign[:], in0=coef_b, scalar1=0.0, scalar2=None, op0=ALU.is_gt)
+            nc.gpsimd.tensor_scalar(out=negative[:], in0=coef_b, scalar1=0.0, scalar2=None, op0=ALU.is_lt)
+            nc.gpsimd.tensor_tensor(out=coef_b_sign[:], in0=coef_b_sign[:], in1=negative[:], op=ALU.subtract)
+            nc.gpsimd.tensor_tensor(out=factor_a[:], in0=coef_a, in1=coef_b_sign[:], op=ALU.mult)
+
+        def head_scales(engine):
+            for half in range(2):
+                b = bank("turn", "spread")
+                for j in range(4):
+                    r = 4 * half + j
+                    nc.tensor.transpose(
+                        b[:, P * j : P * j + P], scale_cols[:, r : r + 1].to_broadcast([P, P]), ident[:]
+                    )
+                copy(engine, scale_all[:, HALF * half : HALF * half + HALF], b[:])
+
+        def head_logarithms():
+            nc.scalar.activation(out=coef_b_ln[:], in_=coef_b_abs[:], func=ACT.Ln)
+            nc.scalar.activation(out=unused[:], in_=coef_b_ln[:, 0:1], func=ACT.Exp)
+
+        qb_prod, turned, kb_mixed, exps, probs = {}, {}, {}, {}, {}
+
+        def multiply(g, t):
+            qb_prod[g, t] = work.tile([P, D], BF16, name="qb_prod", tag="qb_prod", bufs=4, align_bytes=64)
+            nc.vector.tensor_tensor(
+                out=qb_prod[g, t][:], in0=qb_bytes[g][:, t, :].bitcast(FP8), in1=scale_all[:], op=ALU.mult
+            )
 
         def turn(side, g, t, engine):
-            src = qar[g, t // 2][:, t % 2, :] if side == 0 else prod[g, t][:]
-            words = src.bitcast(F32)
-            b = bank("tp", "tb")
-            for c in range(2):
+            rows = qa_raw[g, t // 2][:, t % 2, :] if side == 0 else qb_prod[g, t][:]
+            words = rows.bitcast(F32)
+            b = bank("turn", "turned_words")
+            for c in range(PASSES):
                 for u in range(2):
                     j = 2 * c + u
                     nc.tensor.transpose(
                         b[:, P * j : P * j + P], words[:, 256 * c + u : 256 * c + 256 : 2], ident[:]
                     )
-            if (side, g) not in grp:
-                grp[side, g] = work.tile([P, 4, 2, P, 2], F32, name="grp", tag="grp", bufs=3, align_bytes=64)
-            move(engine, grp[side, g][:, t, :, :, :], b[:].rearrange("p (c u r) -> p c r u", c=2, u=2))
+            if (side, g) not in turned:
+                turned[side, g] = work.tile(
+                    [P, SLOTS, PASSES, P, 2], F32, name="turned", tag="turned", bufs=3, align_bytes=64
+                )
+            copy(engine, turned[side, g][:, t, :, :, :], b[:].rearrange("p (c u r) -> p c r u", c=PASSES, u=2))
 
-        def quant_q(side, g):
+        def quantise_queries(side, g):
             nc.vector.quantize_mx(
-                out=qc[side, g][:].rearrange("p a c r -> p (a c r)").bitcast(E4M3X4),
-                scales=qs[side, g][:].rearrange("p a c r -> p (a c r)"),
-                in_=grp[side, g][:].rearrange("p a c r u -> p (a c r u)").bitcast(BF16),
+                out=q_codes[side, g][:].rearrange("p t c r -> p (t c r)").bitcast(E4M3X4),
+                scales=q_scales[side, g][:].rearrange("p t c r -> p (t c r)"),
+                in_=turned[side, g][:].rearrange("p t c r u -> p (t c r u)").bitcast(BF16),
             )
 
-        def kb_inter(c, h, engine):
-            if h not in kbg:
-                kbg[h] = work.tile([P, 2, 512, 4], BF16, name="kbg", tag="kbg", bufs=1, align_bytes=64)
-            move(
+        def mix_keys(c, half, engine):
+            if half not in kb_mixed:
+                kb_mixed[half] = work.tile(
+                    [P, PASSES, HALF, SLOTS], BF16, name="kb_mixed", tag="kb_mixed", bufs=1, align_bytes=64
+                )
+            copy(
                 engine,
-                kbg[h][:, c, :, :].rearrange("p (c i) t -> p c t i", i=4),
-                kbr[c, h][:].rearrange("p t (c i) -> p c t i", i=4),
+                kb_mixed[half][:, c, :, :].rearrange("p (n i) t -> p n t i", i=4),
+                kb_raw[c, half][:].rearrange("p t (n i) -> p n t i", i=4),
             )
 
-        def kb_quant(h):
+        def quantise_keys(half):
             nc.vector.quantize_mx(
-                out=kbc[:, h, :, :].rearrange("p c n -> p (c n)").bitcast(E4M3X4),
-                scales=kbs[:, h, :, :].rearrange("p c n -> p (c n)"),
-                in_=kbg[h][:].rearrange("p c n t -> p (c n t)"),
+                out=kb_codes[:, half, :, :].rearrange("p c n -> p (c n)").bitcast(E4M3X4),
+                scales=kb_scales[:, half, :, :].rearrange("p c n -> p (c n)"),
+                in_=kb_mixed[half][:].rearrange("p c n t -> p (c n t)"),
             )
 
-        def scores(dst, side, g, t, s0, w):
-            for c in range(2):
+        def score_slot(dst, side, g, t, first, width):
+            for c in range(PASSES):
                 if side == 0:
-                    rhs = kaw[:, c, 2 * s0 : 2 * s0 + 2 * w].bitcast(E2M1X4)
-                    rsc = kas[:, c, s0 : s0 + w]
+                    keys = ka_words[:, c, 2 * first : 2 * (first + width)].bitcast(E2M1X4)
+                    key_scales = ka_scales[:, c, first : first + width]
                 else:
-                    rhs = kbc[:, s0 // 512, c, :].bitcast(E4M3X4)
-                    rsc = kbs[:, s0 // 512, c, :]
+                    keys = kb_codes[:, first // HALF, c, :].bitcast(E4M3X4)
+                    key_scales = kb_scales[:, first // HALF, c, :]
                 nc.tensor.matmul_mx(
                     out=dst,
-                    lhsT=qc[side, g][:, t, c, :].bitcast(E4M3X4),
-                    lhsT_scale=qs[side, g][:, t, c, :],
-                    rhs=rhs,
-                    rhs_scale=rsc,
+                    lhsT=q_codes[side, g][:, t, c, :].bitcast(E4M3X4),
+                    lhsT_scale=q_scales[side, g][:, t, c, :],
+                    rhs=keys,
+                    rhs_scale=key_scales,
                     start=(c == 0),
-                    stop=(c == 1),
+                    stop=(c == PASSES - 1),
                 )
 
-        def score(side, bi, g, t):
-            b = bank("mm", "sc")
-            k = 4 * g + t
-            if side == 0 and bi > 0:
-                for j in range(4):
-                    scores(b[:, P * j : P * j + P], 0, g, j, 384 + P * bi, P)
-                if bi not in ex:
-                    ex[bi] = work.tile([P, GROUPS, P, 4], F32, name="ea", tag="ea", bufs=3, align_bytes=64)
+        def small(side, block):
+            return side == 0 and block > 0
+
+        def score(side, block, g, t):
+            b = bank("mm", "scores")
+            if small(side, block):
+                for j in range(SLOTS):
+                    score_slot(b[:, P * j : P * j + P], 0, g, j, HALF + P * (block - 1), P)
+                if (side, block) not in exps:
+                    exps[side, block] = work.tile(
+                        [P, GROUPS, P, SLOTS], F32, name="exp_a", tag="exp_a", bufs=3, align_bytes=64
+                    )
                 nc.scalar.activation(
-                    out=ex[bi][:, g, :, :], in_=b[:].rearrange("p (t n) -> p n t", t=4), func=ACT.Exp
+                    out=exps[side, block][:, g, :, :], in_=b[:].rearrange("p (t n) -> p n t", t=SLOTS), func=ACT.Exp
                 )
                 return
-            scores(b[:], side, g, t, 512 * bi, 512)
-            if (side, bi, g) not in ex:
-                ex[side, bi, g] = work.tile(
-                    [P, 4, 512], BF16 if side else F32, name="ex", tag="eb" if side else "ea", bufs=3, align_bytes=64
+            score_slot(b[:], side, g, t, HALF * block, HALF)
+            if (side, block, g) not in exps:
+                exps[side, block, g] = work.tile(
+                    [P, SLOTS, HALF],
+                    F32 if side == 0 else BF16,
+                    name="exp_slots",
+                    tag="exp_a" if side == 0 else "exp_b",
+                    bufs=3,
+                    align_bytes=64,
                 )
-            dst = ex[side, bi, g][:, t, :]
+            dst = exps[side, block, g][:, t, :]
             if side == 0:
                 nc.scalar.activation(out=dst, in_=b[:], func=ACT.Exp)
             else:
-                nc.scalar.activation(out=dst, in_=b[:], func=ACT.Exp, bias=lnb[:, k : k + 1])
+                k = SLOTS * g + t
+                nc.scalar.activation(out=dst, in_=b[:], func=ACT.Exp, bias=coef_b_ln[:, k : k + 1])
 
-        def weigh(side, bi, g):
-            if side == 0 and bi > 0:
-                o = work.tile([P, GROUPS, P, 4], BF16, name="pg", tag="pg", bufs=4, align_bytes=64)
+        def weigh(side, block, g):
+            if small(side, block):
+                w = work.tile([P, GROUPS, P, SLOTS], BF16, name="prob", tag="prob", bufs=4, align_bytes=64)
+                factors = factor_a[:].rearrange("p (g t) -> p g t", t=SLOTS).unsqueeze(2)
                 nc.vector.tensor_tensor(
-                    out=o[:],
-                    in0=ex[bi][:],
-                    in1=ca[:]
-                    .rearrange("p (g t) -> p g t", t=4)
-                    .unsqueeze(2)
-                    .to_broadcast([P, GROUPS, P, 4]),
+                    out=w[:],
+                    in0=exps[side, block][:],
+                    in1=factors.to_broadcast([P, GROUPS, P, SLOTS]),
                     op=ALU.mult,
                 )
-                pg[side, bi] = o
+                probs[side, block] = w
                 return
-            o = work.tile([P, 512, 4], BF16, name="pg", tag="pg", bufs=4, align_bytes=64)
-            src = ex[side, bi, g][:].rearrange("p t (c i) -> p c t i", i=4)
-            dst = o[:].rearrange("p (c i) t -> p c t i", i=4)
+            w = work.tile([P, HALF, SLOTS], BF16, name="prob", tag="prob", bufs=4, align_bytes=64)
+            src = exps[side, block, g][:].rearrange("p t (n i) -> p n t i", i=4)
+            dst = w[:].rearrange("p (n i) t -> p n t i", i=4)
             if side == 0:
+                factors = factor_a[:, SLOTS * g : SLOTS * g + SLOTS].unsqueeze(1).unsqueeze(3)
                 nc.vector.tensor_tensor(
-                    out=dst,
-                    in0=src,
-                    in1=ca[:, 4 * g : 4 * g + 4].unsqueeze(1).unsqueeze(3).to_broadcast([P, 128, 4, 4]),
-                    op=ALU.mult,
+                    out=dst, in0=src, in1=factors.to_broadcast([P, HALF // 4, SLOTS, 4]), op=ALU.mult
                 )
             else:
                 nc.vector.tensor_copy(out=dst, in_=src)
-            pg[side, bi, g] = o
+            probs[side, block, g] = w
 
-        def quant_p(side, bi, z):
-            if side == 0 and bi > 0:
-                lo, n = (0, 2) if z == 0 else (2, 1)
-                codes = pak[:, bi - 1, lo : lo + n, :].rearrange("p g n -> p (g n)")
-                scales = pal[:, bi - 1, lo : lo + n, :].rearrange("p g n -> p (g n)")
-                src = pg[side, bi][:, lo : lo + n, :, :].rearrange("p g n t -> p (g n t)")
+        def quantise_probs(side, block, part):
+            if small(side, block):
+                lo, n = (0, 2) if part == 0 else (2, 1)
+                codes = pa_blk_codes[:, block - 1, lo : lo + n, :].rearrange("p g n -> p (g n)")
+                scales = pa_blk_scales[:, block - 1, lo : lo + n, :].rearrange("p g n -> p (g n)")
+                src = probs[side, block][:, lo : lo + n, :, :].rearrange("p g n t -> p (g n t)")
             else:
-                s0 = 512 * bi
-                codes = pbc[:, z, s0 : s0 + 512] if side else pac[:, z, :]
-                scales = pbs[:, z, s0 : s0 + 512] if side else pas[:, z, :]
-                src = pg[side, bi, z][:].rearrange("p n t -> p (n t)")
+                first = HALF * block
+                codes = (pb_codes if side else pa_codes)[:, part, first : first + HALF]
+                scales = (pb_scales if side else pa_scales)[:, part, first : first + HALF]
+                src = probs[side, block, part][:].rearrange("p n t -> p (n t)")
             nc.vector.quantize_mx(out=codes.bitcast(E4M3X4), scales=scales, in_=src)
 
-        def credit(i, bi, engine):
-            b = bank("mm", "cr")
+        def credit(i, half, engine):
+            b = bank("mm", "credit")
             for g in range(GROUPS):
-                if i < 4:
-                    lhsT, lsc = pac[:, g, P * i : P * i + P], pas[:, g, P * i : P * i + P]
+                if i < HALF // P:
+                    rows, row_scales = pa_codes[:, g, P * i : P * i + P], pa_scales[:, g, P * i : P * i + P]
                 else:
-                    lhsT, lsc = pak[:, i - 4, g, :], pal[:, i - 4, g, :]
+                    rows, row_scales = pa_blk_codes[:, i - HALF // P, g, :], pa_blk_scales[:, i - HALF // P, g, :]
                 nc.tensor.matmul_mx(
                     out=b[:],
-                    lhsT=lhsT.bitcast(E4M3X4),
-                    lhsT_scale=lsc,
-                    rhs=pbc[:, g, 512 * bi : 512 * bi + 512].bitcast(E4M3X4),
-                    rhs_scale=pbs[:, g, 512 * bi : 512 * bi + 512],
+                    lhsT=rows.bitcast(E4M3X4),
+                    lhsT_scale=row_scales,
+                    rhs=pb_codes[:, g, HALF * half : HALF * half + HALF].bitcast(E4M3X4),
+                    rhs_scale=pb_scales[:, g, HALF * half : HALF * half + HALF],
                     start=(g == 0),
                     stop=(g == GROUPS - 1),
                 )
-            o = work.tile([P, 512], F32, name="o", tag="o", bufs=4)
-            move(engine, o[:], b[:])
-            nc.sync.dma_start(out=out[P * i : P * i + P, 512 * bi : 512 * bi + 512], in_=o[:])
+            o = work.tile([P, HALF], F32, name="stored", tag="stored", bufs=4)
+            copy(engine, o[:], b[:])
+            nc.sync.dma_start(out=out[P * i : P * i + P, HALF * half : HALF * half + HALF], in_=o[:])
 
-        def emit(u):
-            k = u[0]
-            a = [int(x) for x in u[1:] if x in "0123456789"]
-            e = u[-1]
-            if k == "d":
-                warm_up()
-            elif k == "p":
-                product(*a)
-            elif k == "t":
-                turn(a[0], a[1], a[2], e)
-            elif k == "q":
-                quant_q(a[0], a[1])
-            elif k == "i":
-                kb_inter(a[0], a[1], e)
-            elif k == "j":
-                kb_quant(*a)
-            elif k == "s":
-                score(*a)
-            elif k == "w":
-                weigh(*a)
-            elif k == "x":
-                quant_p(*a)
-            elif k == "c":
-                credit(a[0], a[1], e)
+        def run(step):
+            n = [int(x) for x in step[1:] if x in "0123456789"]
+            engine = step[-1]
+            if step[0] == "d":
+                busy()
+            elif step[0] == "h":
+                if n[0] == 1:
+                    head_columns()
+                elif n[0] == 2:
+                    head_scales(engine)
+                else:
+                    head_logarithms()
+            elif step[0] == "p":
+                multiply(*n)
+            elif step[0] == "t":
+                turn(n[0], n[1], n[2], engine)
+            elif step[0] == "q":
+                quantise_queries(*n)
+            elif step[0] == "i":
+                mix_keys(n[0], n[1], engine)
+            elif step[0] == "j":
+                quantise_keys(*n)
+            elif step[0] == "s":
+                score(*n)
+            elif step[0] == "w":
+                weigh(*n)
+            elif step[0] == "x":
+                quantise_probs(*n)
+            else:
+                credit(n[0], n[1], engine)
 
         with tc.manual_schedule():
-            head()
-            for u in ORDER.split():
-                emit(u)
+            first_loads()
+            for step in ORDER.split():
+                run(step)

from contextlib import ExitStack

import concourse.mybir as mybir
from concourse.masks import make_identity

T, D, E = 1536, 1024, 1024
P = 128
SLOTS = 4
GROUPS = T // (P * SLOTS)
PASSES = D // (P * SLOTS)
HALF = 512
FLOPS = 3 * 2 * T * D * E

F32 = mybir.dt.float32
BF16 = mybir.dt.bfloat16
U32 = mybir.dt.uint32
I32 = mybir.dt.int32
U8 = mybir.dt.uint8
FP8 = mybir.dt.float8_e4m3fn
E4M3X4 = mybir.dt.float8_e4m3fn_x4
E2M1X4 = mybir.dt.float4_e2m1fn_x4
ACT = mybir.ActivationFunctionType
ALU = mybir.AluOpType

BANKS = {"turn": 4, "mm": 4}

LOADS = "k00A k10A a00A a01A b0 a10 w a11 x b1 k01 k11 a20 a21 b2"

ORDER = """
h1 d i00s i10v d d j0 h2s t000s d d d t001s p00 t002s t003s p01 p02 d d h3 t100s q00 p03 t010s d d
p10 t101s p11 t011s s0000 i01v t102s t103s q10 t012s s0001 s0002 t013s p12 t110s t111s s0003 s1000
p13 s1001 p20 s1002 p21 s1003 q01 t112s t113s t020s t021s t120s s0010 p22 s0011 i11v p23 t121s q11
w100 t122s t022s t023s q02 t123s q12 s0012 s0013 j1 s1010 s1011 s1012 s1013 x100 s0020 w000 w001
s0021 x000 s1020 x001 s0022 s1021 s1022 s0023 s1023 s0100 w101 s1100 w102 s1101 s1102 s1103 w002
w110 s0110 s0120 s0200 s1110 s1111 s1112 x101 x102 s1113 s0210 s1120 s1121 s0220 x002 s0300 w010
s1122 w111 s0310 s1123 s0320 w112 x110 x111 s0400 c00s x112 c10s w020 x010 c20s s0410 x011 c30s
s0420 c01s c11s c21s x020 w030 c31s x021 c40s c41s x030 x031 w040 x040 c50s x041 c51s c60v c61s c70s
c71v
"""


def tile_product_key_credit_s11_kernel(
    tc, query_a, query_b_bytes, query_b_scale, keys_a_words, keys_a_scales, keys_b, coef, out
):
    nc = tc.nc
    with ExitStack() as ctx:
        keep = ctx.enter_context(tc.tile_pool(name="keep", bufs=1))
        work = ctx.enter_context(tc.tile_pool(name="work", bufs=2))
        psum = ctx.enter_context(tc.psum_pool(name="psum", bufs=1))

        ident = keep.tile([P, P], F32, name="ident")
        dummy = keep.tile([P, HALF], BF16, name="dummy")
        coef_rows = keep.tile([P, HALF // 2], F32, name="coef_rows")
        scale_rows = keep.tile([P, P], F32, name="scale_rows")
        scale_cols = keep.tile([P, D // P], F32, name="scale_cols")
        scale_all = keep.tile([P, D], F32, name="scale_all", align_bytes=64)
        coefs = keep.tile([P, 2 * GROUPS * SLOTS], F32, name="coefs")
        coef_b_abs = keep.tile([P, GROUPS * SLOTS], F32, name="coef_b_abs")
        coef_b_ln = keep.tile([P, GROUPS * SLOTS], F32, name="coef_b_ln")
        coef_b_sign = keep.tile([P, GROUPS * SLOTS], F32, name="coef_b_sign")
        negative = keep.tile([P, GROUPS * SLOTS], F32, name="negative")
        factor_a = keep.tile([P, GROUPS * SLOTS], F32, name="factor_a")
        unused = keep.tile([P, 1], F32, name="unused")

        ka_words = keep.tile([P, PASSES, 2 * E], U8, name="ka_words", align_bytes=64)
        ka_scales = keep.tile([P, PASSES, E], U8, name="ka_scales", align_bytes=64)
        kb_codes = keep.tile([P, 2, PASSES, HALF], U32, name="kb_codes", align_bytes=64)
        kb_scales = keep.tile([P, 2, PASSES, HALF], U8, name="kb_scales", align_bytes=64)
        pa_codes = keep.tile([P, GROUPS, HALF], U32, name="pa_codes", align_bytes=64)
        pa_scales = keep.tile([P, GROUPS, HALF], U8, name="pa_scales", align_bytes=64)
        pa_blk_codes = keep.tile([P, HALF // P, GROUPS, P], U32, name="pa_blk_codes", align_bytes=64)
        pa_blk_scales = keep.tile([P, HALF // P, GROUPS, P], U8, name="pa_blk_scales", align_bytes=64)
        pb_codes = keep.tile([P, GROUPS, E], U32, name="pb_codes", align_bytes=64)
        pb_scales = keep.tile([P, GROUPS, E], U8, name="pb_scales", align_bytes=64)
        q_codes, q_scales = {}, {}
        for side in range(2):
            for g in range(GROUPS):
                q_codes[side, g] = keep.tile([P, SLOTS, PASSES, P], U32, name="qc%d%d" % (side, g), align_bytes=64)
                q_scales[side, g] = keep.tile([P, SLOTS, PASSES, P], U8, name="qs%d%d" % (side, g), align_bytes=64)
        qb_bytes = [keep.tile([P, SLOTS, D], U8, name="qb_bytes%d" % g, align_bytes=64) for g in range(GROUPS)]
        kb_raw = {}
        for half in range(2):
            for c in range(PASSES):
                kb_raw[c, half] = keep.tile([P, SLOTS, HALF], BF16, name="kb_raw%d%d" % (c, half), align_bytes=64)

        make_identity(nc, ident[:])

        def bank(use, name):
            return psum.tile([P, HALF], F32, name=name, tag=use, bufs=BANKS[use])

        def copy(engine, dst, src):
            if engine == "s":
                nc.scalar.copy(out=dst, in_=src)
            else:
                nc.vector.tensor_copy(out=dst, in_=src)

        qa_view = query_a.rearrange("(g p t) d -> g p t d", p=P, t=SLOTS)
        qb_view = query_b_bytes.rearrange("(g p t) d -> g p t d", p=P, t=SLOTS)
        kb_view = keys_b.rearrange("(c p t) n -> c p t n", p=P, t=SLOTS)
        qa_raw = {}

        def load(step):
            n = [int(x) for x in step[1:] if x in "0123456789"]
            queue = nc.scalar if step[-1] == "A" else nc.sync
            if step[0] == "a":
                g, pair = n
                qa_raw[g, pair] = work.tile([P, 2, D], BF16, name="qa_raw", tag="qa_raw", bufs=5, align_bytes=64)
                queue.dma_start(out=qa_raw[g, pair][:], in_=qa_view[g][:, 2 * pair : 2 * pair + 2, :])
            elif step[0] == "b":
                queue.dma_start(out=qb_bytes[n[0]][:], in_=qb_view[n[0]])
            elif step[0] == "k":
                c, half = n
                queue.dma_start(out=kb_raw[c, half][:], in_=kb_view[c][:, :, HALF * half : HALF * half + HALF])
            elif step[0] == "w":
                queue.dma_start(out=ka_words[:], in_=keys_a_words.rearrange("c p x -> p c x"))
            else:
                for q in range(4):
                    queue.dma_start(
                        out=ka_scales[32 * q : 32 * q + 4, :, :].bitcast(I32),
                        in_=keys_a_scales[:, 4 * q : 4 * q + 4, :].rearrange("c r n -> r c n").bitcast(I32),
                    )

        def first_loads():
            nc.vector.memset(coef_rows[:], 0.0)
            nc.vector.memset(scale_rows[:], 0.0)
            nc.vector.memset(dummy[:], 0.0)
            nc.vector.memset(ka_scales[:].rearrange("p c n -> p (c n)").bitcast(I32), 0)
            rows = coef.rearrange("s (g m) -> (s g) m", m=HALF)
            nc.scalar.dma_start(out=coef_rows[0:4, :].bitcast(BF16), in_=rows[0:4, :])
            nc.scalar.dma_start(out=coef_rows[4:6, :].bitcast(BF16), in_=rows[4:6, :])
            nc.sync.dma_start(out=scale_rows[0 : D // P, :], in_=query_b_scale.rearrange("o (r n) -> (o r) n", n=P))
            for step in LOADS.split():
                load(step)

        def busy():
            b = bank("mm", "busy")
            nc.tensor.matmul(b[:], lhsT=dummy[:, 0:P], rhs=dummy[:], start=True, stop=True)

        def head_columns():
            b = bank("turn", "head")
            nc.tensor.transpose(b[:, 2 * P : 3 * P], scale_rows[:], ident[:])
            for u in range(2):
                nc.tensor.transpose(b[:, P * u : P * u + P], coef_rows[:, u::2], ident[:])
            nc.vector.tensor_copy(out=scale_cols[:], in_=b[:, 2 * P : 2 * P + D // P])
            nc.vector.tensor_copy(
                out=coefs[:].rearrange("p (x u e) -> p u x e", u=2, e=2),
                in_=b[:, 0 : 2 * P].bitcast(BF16).rearrange("p (u r e) -> p u r e", u=2, e=2)[:, :, 0 : 2 * GROUPS, :],
            )
            coef_a = coefs[:, 0 : GROUPS * SLOTS]
            coef_b = coefs[:, GROUPS * SLOTS : 2 * GROUPS * SLOTS]
            nc.vector.scalar_tensor_tensor(
                out=coef_b_abs[:], in0=coef_b, scalar=-1.0, in1=coef_b, op0=ALU.mult, op1=ALU.max
            )
            nc.vector.tensor_scalar(
                out=coef_b_abs[:], in0=coef_b_abs[:], scalar1=1e-19, scalar2=None, op0=ALU.max
            )
            nc.gpsimd.tensor_scalar(out=coef_b_sign[:], in0=coef_b, scalar1=0.0, scalar2=None, op0=ALU.is_gt)
            nc.gpsimd.tensor_scalar(out=negative[:], in0=coef_b, scalar1=0.0, scalar2=None, op0=ALU.is_lt)
            nc.gpsimd.tensor_tensor(out=coef_b_sign[:], in0=coef_b_sign[:], in1=negative[:], op=ALU.subtract)
            nc.gpsimd.tensor_tensor(out=factor_a[:], in0=coef_a, in1=coef_b_sign[:], op=ALU.mult)

        def head_scales(engine):
            for half in range(2):
                b = bank("turn", "spread")
                for j in range(4):
                    r = 4 * half + j
                    nc.tensor.transpose(
                        b[:, P * j : P * j + P], scale_cols[:, r : r + 1].to_broadcast([P, P]), ident[:]
                    )
                copy(engine, scale_all[:, HALF * half : HALF * half + HALF], b[:])

        def head_logarithms():
            nc.scalar.activation(out=coef_b_ln[:], in_=coef_b_abs[:], func=ACT.Ln)
            nc.scalar.activation(out=unused[:], in_=coef_b_ln[:, 0:1], func=ACT.Exp)

        qb_prod, turned, kb_mixed, exps, probs = {}, {}, {}, {}, {}

        def multiply(g, t):
            qb_prod[g, t] = work.tile([P, D], BF16, name="qb_prod", tag="qb_prod", bufs=4, align_bytes=64)
            nc.vector.tensor_tensor(
                out=qb_prod[g, t][:], in0=qb_bytes[g][:, t, :].bitcast(FP8), in1=scale_all[:], op=ALU.mult
            )

        def turn(side, g, t, engine):
            rows = qa_raw[g, t // 2][:, t % 2, :] if side == 0 else qb_prod[g, t][:]
            words = rows.bitcast(F32)
            b = bank("turn", "turned_words")
            for c in range(PASSES):
                for u in range(2):
                    j = 2 * c + u
                    nc.tensor.transpose(
                        b[:, P * j : P * j + P], words[:, 256 * c + u : 256 * c + 256 : 2], ident[:]
                    )
            if (side, g) not in turned:
                turned[side, g] = work.tile(
                    [P, SLOTS, PASSES, P, 2], F32, name="turned", tag="turned", bufs=3, align_bytes=64
                )
            copy(engine, turned[side, g][:, t, :, :, :], b[:].rearrange("p (c u r) -> p c r u", c=PASSES, u=2))

        def quantise_queries(side, g):
            nc.vector.quantize_mx(
                out=q_codes[side, g][:].rearrange("p t c r -> p (t c r)").bitcast(E4M3X4),
                scales=q_scales[side, g][:].rearrange("p t c r -> p (t c r)"),
                in_=turned[side, g][:].rearrange("p t c r u -> p (t c r u)").bitcast(BF16),
            )

        def mix_keys(c, half, engine):
            if half not in kb_mixed:
                kb_mixed[half] = work.tile(
                    [P, PASSES, HALF, SLOTS], BF16, name="kb_mixed", tag="kb_mixed", bufs=1, align_bytes=64
                )
            copy(
                engine,
                kb_mixed[half][:, c, :, :].rearrange("p (n i) t -> p n t i", i=4),
                kb_raw[c, half][:].rearrange("p t (n i) -> p n t i", i=4),
            )

        def quantise_keys(half):
            nc.vector.quantize_mx(
                out=kb_codes[:, half, :, :].rearrange("p c n -> p (c n)").bitcast(E4M3X4),
                scales=kb_scales[:, half, :, :].rearrange("p c n -> p (c n)"),
                in_=kb_mixed[half][:].rearrange("p c n t -> p (c n t)"),
            )

        def score_slot(dst, side, g, t, first, width):
            for c in range(PASSES):
                if side == 0:
                    keys = ka_words[:, c, 2 * first : 2 * (first + width)].bitcast(E2M1X4)
                    key_scales = ka_scales[:, c, first : first + width]
                else:
                    keys = kb_codes[:, first // HALF, c, :].bitcast(E4M3X4)
                    key_scales = kb_scales[:, first // HALF, c, :]
                nc.tensor.matmul_mx(
                    out=dst,
                    lhsT=q_codes[side, g][:, t, c, :].bitcast(E4M3X4),
                    lhsT_scale=q_scales[side, g][:, t, c, :],
                    rhs=keys,
                    rhs_scale=key_scales,
                    start=(c == 0),
                    stop=(c == PASSES - 1),
                )

        def small(side, block):
            return side == 0 and block > 0

        def score(side, block, g, t):
            b = bank("mm", "scores")
            if small(side, block):
                for j in range(SLOTS):
                    score_slot(b[:, P * j : P * j + P], 0, g, j, HALF + P * (block - 1), P)
                if (side, block) not in exps:
                    exps[side, block] = work.tile(
                        [P, GROUPS, P, SLOTS], F32, name="exp_a", tag="exp_a", bufs=3, align_bytes=64
                    )
                nc.scalar.activation(
                    out=exps[side, block][:, g, :, :], in_=b[:].rearrange("p (t n) -> p n t", t=SLOTS), func=ACT.Exp
                )
                return
            score_slot(b[:], side, g, t, HALF * block, HALF)
            if (side, block, g) not in exps:
                exps[side, block, g] = work.tile(
                    [P, SLOTS, HALF],
                    F32 if side == 0 else BF16,
                    name="exp_slots",
                    tag="exp_a" if side == 0 else "exp_b",
                    bufs=3,
                    align_bytes=64,
                )
            dst = exps[side, block, g][:, t, :]
            if side == 0:
                nc.scalar.activation(out=dst, in_=b[:], func=ACT.Exp)
            else:
                k = SLOTS * g + t
                nc.scalar.activation(out=dst, in_=b[:], func=ACT.Exp, bias=coef_b_ln[:, k : k + 1])

        def weigh(side, block, g):
            if small(side, block):
                w = work.tile([P, GROUPS, P, SLOTS], BF16, name="prob", tag="prob", bufs=4, align_bytes=64)
                factors = factor_a[:].rearrange("p (g t) -> p g t", t=SLOTS).unsqueeze(2)
                nc.vector.tensor_tensor(
                    out=w[:],
                    in0=exps[side, block][:],
                    in1=factors.to_broadcast([P, GROUPS, P, SLOTS]),
                    op=ALU.mult,
                )
                probs[side, block] = w
                return
            w = work.tile([P, HALF, SLOTS], BF16, name="prob", tag="prob", bufs=4, align_bytes=64)
            src = exps[side, block, g][:].rearrange("p t (n i) -> p n t i", i=4)
            dst = w[:].rearrange("p (n i) t -> p n t i", i=4)
            if side == 0:
                factors = factor_a[:, SLOTS * g : SLOTS * g + SLOTS].unsqueeze(1).unsqueeze(3)
                nc.vector.tensor_tensor(
                    out=dst, in0=src, in1=factors.to_broadcast([P, HALF // 4, SLOTS, 4]), op=ALU.mult
                )
            else:
                nc.vector.tensor_copy(out=dst, in_=src)
            probs[side, block, g] = w

        def quantise_probs(side, block, part):
            if small(side, block):
                lo, n = (0, 2) if part == 0 else (2, 1)
                codes = pa_blk_codes[:, block - 1, lo : lo + n, :].rearrange("p g n -> p (g n)")
                scales = pa_blk_scales[:, block - 1, lo : lo + n, :].rearrange("p g n -> p (g n)")
                src = probs[side, block][:, lo : lo + n, :, :].rearrange("p g n t -> p (g n t)")
            else:
                first = HALF * block
                codes = (pb_codes if side else pa_codes)[:, part, first : first + HALF]
                scales = (pb_scales if side else pa_scales)[:, part, first : first + HALF]
                src = probs[side, block, part][:].rearrange("p n t -> p (n t)")
            nc.vector.quantize_mx(out=codes.bitcast(E4M3X4), scales=scales, in_=src)

        def credit(i, half, engine):
            b = bank("mm", "credit")
            for g in range(GROUPS):
                if i < HALF // P:
                    rows, row_scales = pa_codes[:, g, P * i : P * i + P], pa_scales[:, g, P * i : P * i + P]
                else:
                    rows, row_scales = pa_blk_codes[:, i - HALF // P, g, :], pa_blk_scales[:, i - HALF // P, g, :]
                nc.tensor.matmul_mx(
                    out=b[:],
                    lhsT=rows.bitcast(E4M3X4),
                    lhsT_scale=row_scales,
                    rhs=pb_codes[:, g, HALF * half : HALF * half + HALF].bitcast(E4M3X4),
                    rhs_scale=pb_scales[:, g, HALF * half : HALF * half + HALF],
                    start=(g == 0),
                    stop=(g == GROUPS - 1),
                )
            o = work.tile([P, HALF], F32, name="stored", tag="stored", bufs=4)
            copy(engine, o[:], b[:])
            nc.sync.dma_start(out=out[P * i : P * i + P, HALF * half : HALF * half + HALF], in_=o[:])

        def run(step):
            n = [int(x) for x in step[1:] if x in "0123456789"]
            engine = step[-1]
            if step[0] == "d":
                busy()
            elif step[0] == "h":
                if n[0] == 1:
                    head_columns()
                elif n[0] == 2:
                    head_scales(engine)
                else:
                    head_logarithms()
            elif step[0] == "p":
                multiply(*n)
            elif step[0] == "t":
                turn(n[0], n[1], n[2], engine)
            elif step[0] == "q":
                quantise_queries(*n)
            elif step[0] == "i":
                mix_keys(n[0], n[1], engine)
            elif step[0] == "j":
                quantise_keys(*n)
            elif step[0] == "s":
                score(*n)
            elif step[0] == "w":
                weigh(*n)
            elif step[0] == "x":
                quantise_probs(*n)
            else:
                credit(n[0], n[1], engine)

        with tc.manual_schedule():
            first_loads()
            for step in ORDER.split():
                run(step)
